import numpy as np, ml_dtypes
CORES = [3,11,19,27,35,43,51,59]
N = 8
BF = ml_dtypes.bfloat16
def gentries(a):
    return np.ascontiguousarray(a.reshape(8, 16, -1).transpose(0, 2, 1)).reshape(8, -1)
def gtable(e):
    e = np.asarray(e); return np.ascontiguousarray(e.reshape(8, -1, 16).transpose(0, 2, 1)).reshape(128, -1).astype(np.int32)
V, CAP, RO, DEC = 256, 32, 3, 24
S = N * V; E = 16 * S; D = 16 * N
def level(rng, *shape):
    return (256 * rng.random(shape[:2] + (1,) + shape[3:]) * rng.random(shape)).astype(np.int64)
def parts(rng):
    fan = np.argsort(rng.random((N, 8, E)), axis=-1)
    lo = rng.choice(np.array([0, 32, 96]), (N, 8, 1)); cost = lo + ((256 - lo) * rng.random((N, 8, E))).astype(np.int64)
    th = np.stack([rng.permutation(np.array([120, 250, 500, 900, 1300, 1600, 1800, 2000])) for q in range(N)]) + rng.integers(0, 40, (N, 8))
    x = level(rng, N, 8, 16, V); dv = np.where(rng.random((N, 8, 1, RO, V)) < 0.15, level(rng, N, 8, 16, RO, V), 0)
    return x, fan, cost, th, dv
def pack(x, fan, cost, th, dv):
    return {"x0": np.ascontiguousarray(x.reshape(N, 128, V)).astype(np.int32), "fan": np.stack([gtable(a) for a in fan]), "cost": np.ascontiguousarray(cost).astype(np.int32),
            "th": np.ascontiguousarray(np.repeat(th, 16, axis=1)[:, :, None]).astype(np.int32), "drv": np.ascontiguousarray(dv.reshape(N, 128, RO * V)).astype(np.int32)}
def setup_inputs(rng):
    return pack(*parts(rng))
def setup_inputs_room(rng):
    x, fan, cost, th, dv = parts(rng); th = rng.integers(200, 1501, (N, 8)); dv[:, :, :, 0] = 0
    for q in range(N):
        for g in range(8):
            o = rng.permutation(V); t = int(th[q, g]); n = int(rng.choice(np.array([0, 1, CAP - 1, CAP, CAP + 1, V])))
            if q == 0: n = (CAP, CAP + 1, V, CAP - 1, 1, 0, CAP, CAP + 1)[g]
            x[q, g][:, o[:n]] = DEC + (t + 15) // 16 + rng.integers(0, 100, (16, n))
            x[q, g][:, o[n:]] = rng.integers(0, DEC + (t - 1) // 16 + 1, (16, V - n))
    return pack(x, fan, cost, th, dv)
def setup_inputs_ties(rng):
    x, fan, cost, th, dv = parts(rng); th = rng.choice(np.array([1, 2, 15, 16, 17, 255, 1000, 3000]), (N, 8))
    share = np.where(np.arange(8) % 2 == 0, 0.7, 0.1)[None, :, None, None]
    goal = th[:, :, None, None] - 1 + np.where(rng.random((N, 8, 1, V)) < share, rng.integers(1, 3, (N, 8, 1, V)), 0)
    m = goal // 16; y = m + (np.arange(16)[:, None] < goal % 16)
    d = ((np.minimum(m, 254 - DEC - m) + 1) * rng.random((N, 8, 8, V))).astype(np.int64)
    y[:, :, :8] += d; y[:, :, 8:] -= d
    x = np.where(y > 0, y + DEC, rng.integers(0, DEC + 1, y.shape)); dv[:, :, :, 0] = 0
    th[:, 0] = 16 * DEC; th[:, 1] = 16 * DEC + 1
    x[:, :2] = rng.integers(RO * DEC + 1, 256, (N, 2, 16, V)); cost[:, :2] = 255; dv[:, :2] = 0
    x[:, 7] = 0; dv[:, 7] = 0; cost[:, 7] = rng.integers(254, 256, (N, E))
    for q in range(N):
        t = (4080, 4079, 4077, 2049)[q % 4]; th[q, 7] = t; o = rng.permutation(V)[:CAP]
        w = np.repeat(np.array([t - 1, t, 4080]), [CAP // 2, CAP // 4, CAP - CAP // 2 - CAP // 4])
        dv[q, 7][:, 0][:, o] = w // 16 + (np.arange(16)[:, None] < w % 16)
    return pack(x, fan, cost, th, dv)
def setup_inputs_alike(rng):
    x, fan, cost, th, dv = parts(rng); ar = np.arange(E); s = ar // 16; i = ar % 16
    fan[:, 0] = ar; fan[:, 1] = ar[::-1]; fan[:, 2] = (16 * (s // V) + i) * V + s % V
    for q in range(N): fan[q, 3] = (16 * rng.permutation(S)[:, None] + np.arange(16)).reshape(-1)
    fan[:, 5] = fan[0, 5].copy()
    cost[:, ::2] = rng.choice(np.array([0, 1, 254, 255]), (N, 4, E))
    c = cost[:, 2].reshape(N, D, V).copy(); h = c[:, :, ::2].shape[2]
    c[:, :D - 4, ::2] = rng.integers(254, 256, (N, D - 4, h)); c[:, D - 4:, ::2] = rng.integers(0, 2, (N, 4, h))
    cost[:, 2] = c.reshape(N, E); dv[:, 2, :, :, 0] = 0
    x = rng.choice(np.array([0, DEC - 1, DEC, DEC + 1, 128, 255]), (N, 8, 16, V)); x[..., 0] = 255; x[..., V - 1] = 255
    th = rng.choice(np.array([1, 16, 300, 600]), (N, 8)); th[:, 0] = 1; th[N - 1, 7] = 600
    return pack(x, fan, cost, th, dv)
def setup_inputs_quiet(rng):
    x, fan, cost, th, dv = parts(rng); x = np.minimum(x, 254); dv = np.minimum(dv, 254); h = rng.permutation(8); q = rng.permutation(N)
    th[q[0]] = 1; th[:, h[1]] = 1; th[q[1]] = 4080; th[q[1], h[2]] = 1; th[:, h[0]] = 4080
    x[:, h[1]] = 0; dv[:, h[1]] = 0; dv[q[0], h[1], :, 0, V - 1] = 254
    a = int(h[3]); x[:, a] = 0; dv[:, a, :, :2] = 0
    dv[:, a, :, 2] = np.where(rng.random((N, 1, V)) < 0.3, rng.integers(130, 255, (N, 16, V)), 0)
    b = int(h[4]); x[:, b] = 0; dv[:, b] = 0; cost[:, b] = rng.integers(200, 256, (N, E))
    th[:, b] = rng.integers(1000, 1601, N); th[q[1], b] = 4080; k = max(RO - 4, 0)
    for r in range(N):
        n = int(rng.integers(CAP // 2, CAP + 1)); o = rng.permutation(V)[:n]
        dv[r, b][:, k][:, o] = rng.integers(100, 121, (16, n)); dv[r, b][:, k + 1][:, o] = rng.integers(230, 255, (16, n))
    return pack(x, fan, cost, th, dv)
def setup_inputs_spread(rng):
    x, fan, cost, th, dv = parts(rng)
    x = np.minimum((np.exp2(8 * rng.random((N, 8, 1, V))) * rng.random((N, 8, 16, V))).astype(np.int64), 255)
    w = np.exp2(8 * rng.random((N, 8, E))); cost = np.minimum(np.where(rng.random((N, 8, E)) < 0.5, w - 1, 256 - w).astype(np.int64), 255)
    th = np.minimum(np.maximum(np.exp2(12 * rng.random((N, 8))).astype(np.int64), 1), 4080)
    v = np.minimum((np.exp2(8 * rng.random((N, 8, 1, RO, V))) * rng.random((N, 8, 16, RO, V))).astype(np.int64), 255)
    dv = np.where(rng.random((N, 8, 1, RO, V)) < 0.5 * rng.random((N, 8, 1, RO, 1)), v, 0)
    return pack(x, fan, cost, th, dv)
def check_inputs(d):
    bad = []
    for k, lo, hi in (("x0", 0, 255), ("fan", 0, E - 1), ("cost", 0, 255), ("th", 1, 4080), ("drv", 0, 255)):
        if np.min(d[k]) < lo or np.max(d[k]) > hi: bad.append("range of " + k)
    if not all(np.array_equal(np.sort(gentries(a), axis=1), np.tile(np.arange(E), (8, 1))) for a in d["fan"]): bad.append("every slot once in fan")
    t = d["th"].reshape(-1, 16)
    if np.any(t != t[:, :1]): bad.append("th alike in a group")
    return bad
def reference(x0, fan, cost, th, drv):
    x = x0.astype(np.int64).reshape(N, 8, 16, V); t = th.astype(np.int64).reshape(N, 8, 16)[:, :, :1]; dv = drv.astype(np.int64).reshape(N, 8, 16, RO, V)
    c = cost.astype(np.int16).reshape(N, 8, 1, D, V)
    fl = np.stack([gentries(a) for a in fan]).astype(np.int64).reshape(N, 8, S, 16)
    slots = np.zeros((N, 8, 16, E), np.int16); last = np.zeros((N, 8, 16, V), np.int64)
    for k in range(RO):
        best = np.stack([np.max(slots[r].reshape(8, 16, D, V) - c[r], axis=2) for r in range(N)]).astype(np.int64)
        x = np.maximum(np.maximum(x - DEC, dv[:, :, :, k]), np.maximum(best, 0))
        changed = np.add.reduce(np.abs(x - last), axis=2) >= t
        h = changed.astype(np.int64); sent = changed & (np.add.accumulate(h, axis=2) - h < CAP)
        last = np.where(sent[:, :, None, :], x, last)
        for g in range(8):
            s = np.flatnonzero(sent[:, g].reshape(-1))
            col = x[:, g].transpose(1, 0, 2).reshape(16, S)[:, s].astype(np.int16)
            for r in range(N):
                slots[r, g][:, fl[r, g][s]] = col[:, :, None]
    return {"yx": x.reshape(N, 128, V).astype(np.float32), "yl": last.reshape(N, 128, V).astype(np.float32)}

@@ -1,0 +1,294 @@
+from concourse.bass import DstId, RemoteDMATransfer
+from concourse.mybir import AluOpType as A, AxisListType, ActivationFunctionType as F
+
+N, V, CAP, RO, DEC = 8, 256, 32, 3, 24
+P = 128
+W = V * P
+Z = -255.0
+U = W // 16
+PIECES = ((0, 96), (96, 192), (192, 256))
+MP = 96
+L = V + CAP
+NA = 9
+NO = 8
+MSG = {"m0": (0, (1, 2, 3, 4, 5, 6, 7, 0)), "m1": (1, (1, 2, 3, 4, 5, 6, 7))}
+X, K, C, Q, B = 16511.5, 128.0 / 32769.0, 12582912.0, 32769.0, 16383.248046875
+F32, BF, I32, U16 = "float32", "bfloat16", "int32", "uint16"
+
+SCRATCH = {}
+for _n, _m, _t in (
+        ("x0i", V, I32), ("dri", RO * V, I32), ("thi", 1, I32), ("thf", 1, F32), ("th0", 1, F32), ("drs", RO * V, BF),
+        ("fani", 2048, I32), ("sel", 2048, BF), ("ones", 512, BF), ("nones", 128, BF), ("ns", 128, BF), ("bt", 128, BF),
+        ("b1", 128, BF), ("b2", 128, BF), ("bm", 128, BF), ("d0", W, BF), ("d1", W, BF), ("so", MP * P, BF),
+        ("pi", 2, I32), ("jc", 1, F32), ("jb", 1, F32), ("c33", L, BF), ("xe", L, BF), ("la", L, BF), ("a0", V, BF), ("mx", V, BF),
+        ("chg", L, BF), ("cum", L, BF), ("le", L, BF), ("sg", L, BF), ("acc", 1, F32), ("cnt", 2, F32), ("tt2", 2, F32), ("raw", 2, U16),
+        ("sb0", CAP + 2, BF), ("sb1", CAP + 2, BF), ("wo", CAP, F32), ("ho", CAP, F32), ("dd", CAP, F32), ("ido", 2, U16),
+        ("ofo", CAP, U16), ("exo", CAP * 16, BF), ("l32", L, F32), ("x32", V, F32), ("v32", CAP, F32)):
+    SCRATCH[_n] = ("sbuf", [128, _m], _t)
+SCRATCH["ci"] = ("sbuf", [128, 8, V], I32)
+SCRATCH["rc"] = ("sbuf", [128, V, 9], BF)
+for _n, _m in (("pd0", 1536), ("pd1", 1536), ("ps", 512), ("pt", 512)):
+    SCRATCH[_n] = ("psum", [128, _m], F32)
+for _n, (_k, _s) in MSG.items():
+    _m = len(_s)
+    SCRATCH["land" + _n] = ("sbuf", [128, _m, CAP + 2], BF)
+    for _b in ("base", "idf"):
+        SCRATCH[_b + _n] = ("sbuf", [128, _m, 2], F32)
+    SCRATCH["ids" + _n] = ("sbuf", [128, 2 * _m], U16)
+    for _b in ("w", "h", "d"):
+        SCRATCH[_b + _n] = ("sbuf", [128, _m * CAP], F32)
+    SCRATCH["of" + _n] = ("sbuf", [128, _m * CAP], U16)
+    SCRATCH["ex" + _n] = ("sbuf", [128, _m * CAP * 16], BF)
+DMAS = ["dx", "dd0", "dth", "dfan", "dd1", "down", "dyx", "dyl"] + ["dc%d" % q for q in range(8)] + ["dz%d" % u for u in range(16)]
+SEMAPHORES = ["v", "a", "p", "q"] + ["arr" + n for n in MSG] + ["sent" + n for n in MSG] + DMAS
+
+
+def rank_program(g, core, T, topo):
+    r = T.rank_of(core)
+    if r is None:
+        return
+    eng = {"v": g.vector, "a": g.scalar, "p": g.tensor, "q": g, "s": g.sync}
+    cnt, lw, lr, seen = {}, {}, {}, {e: {} for e in eng}
+
+    def need(e, deps):
+        for s in sorted(deps):
+            if seen[e].get(s, 0) < deps[s]:
+                eng[e].wait_ge(T.sem[s], deps[s])
+                seen[e][s] = deps[s]
+
+    def op(e, fn, rd, wr, sem=None, inc=1):
+        deps = {}
+        own = e if sem is None else None
+        for k in rd:
+            if k in lw:
+                s, c = lw[k]
+                deps[s] = max(deps.get(s, 0), c)
+        for k in wr:
+            if k in lw and not (e == "p" and lw[k][0] == "p"):
+                s, c = lw[k]
+                deps[s] = max(deps.get(s, 0), c)
+            for s, c in lr.get(k, {}).items():
+                if s != own:
+                    deps[s] = max(deps.get(s, 0), c)
+        need(e, deps)
+        ins = fn()
+        s = sem or e
+        cnt[s] = cnt.get(s, 0) + inc
+        ins.then_inc(T.sem[s], inc)
+        for k in rd:
+            lr.setdefault(k, {})[s] = cnt[s]
+        for k in wr:
+            lw[k] = (s, cnt[s])
+            lr[k] = {}
+
+    v, a, t = g.vector, g.scalar, g.tensor
+    zk = ["z%d" % u for u in range(16)]
+
+    def zu(u, n=1):
+        return T.d1[:, u * U:(u + n) * U]
+
+    def dma(e, out, in_, rd, wr, sem):
+        op(e, lambda: eng[e].dma_start(out, in_), rd, wr, sem, 16)
+
+    def zdma(us):
+        for u in us:
+            dma("s", zu(u), zu(0), ["z0"], ["z%d" % u], "dz%d" % u)
+
+    def zact(us):
+        for u in us:
+            op("a", lambda: a.activation(zu(u), zu(0), F.Copy), ["z0"], ["z%d" % u])
+
+    dma("s", T.x0i[:], T.x0[:], [], ["x0i"], "dx")
+    dma("s", T.dri[:, 0:V], T.drv[:, 0:V], [], ["dri0"], "dd0")
+    dma("s", T.thi[:], T.th[:], [], ["thi"], "dth")
+    for q in (0, 7, 6, 5, 4, 3, 2, 1):
+        dma("s", T.ci[:, q, :], T.cost[:, 16 * V * q:16 * V * (q + 1)], [], ["ci%d" % q], "dc%d" % q)
+    dma("s", T.dri[:, V:3 * V], T.drv[:, V:3 * V], [], ["dri1"], "dd1")
+    dma("s", T.fani[:], T.fan[:], [], ["fan"], "dfan")
+
+    op("v", lambda: v.memset(T.ones[:], 1.0), [], ["ones"])
+    op("q", lambda: g.affine_select(T.bt[:], T.ones[:, 0:128], [[-16, 8], [0, 16]], A.is_ge, 0.0, 0, 1), ["ones"], ["bt"])
+    op("q", lambda: g.affine_select(T.b1[:], T.bt[:], [[16, 8], [0, 16]], A.is_ge, 0.0, 15, -1), ["bt"], ["b1"])
+    op("q", lambda: g.iota(T.pi[:, 0:1], [[0, 1]], 0, 1), [], ["pi0"])
+
+    def select(k):
+        op("q", lambda: g.affine_select(T.sel[:, 512 * k:512 * k + 512], T.ones[:], [[-1, 4], [-16, 8], [0, 16]], A.is_equal, 0.0, -4 * k, 1),
+           ["ones"], ["sel%d" % k])
+        m = 3 if k == 3 else 4
+        s = T.sel[:, 512 * k:512 * k + 128 * m]
+        op("q", lambda: g.affine_select(s, s, [[-1, m], [-16, 8], [0, 16]], A.not_equal, -1.0, -4 * k - 1, 1), ["sel%d" % k], ["sel%d" % k])
+
+    op("v", lambda: v.memset(zu(0), Z), [], ["z0"])
+    op("v", lambda: v.memset(T.nones[:], -1.0), [], ["nones"])
+    op("q", lambda: g.affine_select(T.ns[:], T.nones[:], [[-16, 8], [0, 16]], A.is_equal, 0.0, 0, 1), ["nones"], ["ns"])
+    select(3)
+    select(1)
+    op("v", lambda: v.memset(T.c33[:], float(CAP + 1)), [], ["c33"])
+    op("v", lambda: v.memset(T.xe[:, V:L], Z), [], ["xp"])
+    op("v", lambda: v.tensor_scalar(T.pi[:, 1:2], T.pi[:, 0:1], 15, None, A.bitwise_and), ["pi0"], ["pi1"])
+    op("v", lambda: v.tensor_scalar(T.jc[:], T.pi[:, 1:2], 16.0, None, A.add), ["pi1"], ["jc"])
+    op("v", lambda: v.tensor_scalar(T.jb[:], T.pi[:, 1:2], 0.5, None, A.add), ["pi1"], ["jb"])
+    op("v", lambda: v.memset(T.rc[:, :, 0], 1024.0), [], ["rc0"])
+    op("v", lambda: v.memset(T.la[:], Z), [], ["la"])
+    zact((1, 2))
+    zdma((5, 6, 7))
+
+    def choose(k, last):
+        th, tk = (T.th0, "th0") if k == 0 else (T.thf, "thf")
+        op("v", lambda: v.tensor_scalar(T.chg[:, 0:V], T.ps[:, 0:V], th[:, 0:1], None, A.is_ge), ["ps", tk], ["chg"])
+        op("v", lambda: v.tensor_scalar(T.chg[:, V:L], T.ps[:, 0:CAP], th[:, 0:1], None, A.is_lt), ["ps", tk], ["chp"])
+        op("v", lambda: v.tensor_tensor_scan(T.cum[:], T.chg[:], T.c33[:], 0.0, A.add, A.min), ["chg", "chp", "c33"], ["cum"])
+        op("a", lambda: a.activation(T.sg[:], T.cum[:], F.Sign, bias=T.jb[:, 0:1], scale=-1.0, accum_out=T.acc[:]), ["cum", "jb"], ["sg", "acc"])
+        op("v", lambda: v.tensor_scalar(T.le[:], T.cum[:], T.jc[:, 0:1], None, A.is_le), ["cum", "jc"], ["le"])
+        op("v", lambda: v.tensor_reduce(T.cnt[:, 1:2], T.le[:], AxisListType.X, A.add), ["le"], ["cnt1"])
+        op("v", lambda: v.tensor_scalar(T.raw[:, 0:1], T.acc[:], 0.5, L / 2.0, A.mult, A.add), ["acc"], ["raw0"])
+        op("v", lambda: v.tensor_copy(T.raw[:, 1:2], T.cnt[:, 1:2]), ["cnt1"], ["raw1"])
+        if last:
+            op("v", lambda: v.tensor_scalar(T.v32[:], T.xe[:, 0:L].indirect(T.raw[:, 0:2]), -Z, None, A.add), ["x", "xp", "raw0", "raw1"], ["v32"])
+            return
+        sb = T["sb%d" % k]
+        op("v", lambda: v.tensor_scalar(T.cnt[:, 0:1], T.acc[:], 0.5, L / 2.0, A.mult, A.add), ["acc"], ["cnt0"])
+        op("v", lambda: v.tensor_copy(sb[:, 0:CAP], T.xe[:, 0:L].indirect(T.raw[:, 0:2])), ["x", "xp", "raw0", "raw1"], ["sbv%d" % k])
+        op("v", lambda: v.tensor_scalar(T.tt2[:], T.cnt[:], float(V), -float(V), A.is_ge, A.mult), ["cnt0", "cnt1"], ["tt2"])
+        op("v", lambda: v.tensor_tensor(sb[:, CAP:CAP + 2], T.cnt[:], T.tt2[:], A.add), ["cnt0", "cnt1", "tt2"], ["sbi%d" % k])
+
+    def send(name):
+        k, shifts = MSG[name]
+        sb = T["sb%d" % k]
+        need("q", {"v": max(lw["sbv%d" % k][1], lw["sbi%d" % k][1])})
+        ids, dsts, n = [], [], 0
+        for i, s in enumerate(shifts):
+            if s == 0:
+                continue
+            rid, pid, _ = topo.addr(T.cores[(r + s) % N])
+            ids.append(DstId(rid=rid, pnc=pid))
+            dsts.append(T["land" + name][:, i, :])
+            n += len(topo.engines(T.cores[(r - s) % N], core))
+        peer = T.cores[(r + 1) % N]
+        g.remote_dma_fused([RemoteDMATransfer(dst_ids=ids, dma_engine_mask=topo.mask(core, peer), remote_sem=T.sem["arr" + name], srcs=[sb[:]], dsts=dsts)],
+                           local_sem=T.sem["sent" + name])
+        cnt["sent" + name] = len(topo.engines(core, peer))
+        cnt["arr" + name] = n
+        lw["land" + name] = ("arr" + name, n)
+
+    def scatter(n, idops, ids, w, h, d, of, copies, exk, e16, tag):
+        steps = idops + [
+            lambda: op("v", lambda: v.tensor_scalar(w[:], T.fani[:, 0:2048].indirect(ids[:, 0:n // 16]), X, K, A.subtract, A.mult), ["fan", "ids" + tag], ["w" + tag]),
+            lambda: op("v", lambda: v.tensor_scalar(h[:], w[:], C, C, A.add, A.subtract), ["w" + tag], ["h" + tag]),
+            lambda: op("v", lambda: v.tensor_tensor(d[:], w[:], h[:], A.subtract), ["w" + tag, "h" + tag], ["d" + tag]),
+            lambda: op("v", lambda: v.tensor_scalar(of[:], d[:], Q, B, A.mult, A.add), ["d" + tag], ["of" + tag])]
+        done = 0
+        for i, step in enumerate(steps):
+            step()
+            upto = len(copies) * (i + 1) // len(steps)
+            for c in copies[done:upto]:
+                c()
+            done = upto
+        op("v", lambda: v.tensor_copy(T.d1[:, 0:W].indirect(of[:, 0:n]), e16[:]), ["of" + tag] + exk, zk)
+
+    def own(k):
+        sb, sv = T["sb%d" % k], "sbv%d" % k
+        exk = ["exo%d" % i for i in range(16)]
+        for i in range(NO):
+            op("a", lambda: a.activation(T.exo[:, i::16], sb[:, 0:CAP], F.Copy), [sv], [exk[i]])
+        idops = [lambda: op("v", lambda: v.tensor_scalar(T.ido[:], sb[:, CAP:CAP + 2], float(V * r), None, A.add), ["sbi%d" % k], ["idso"])]
+        copies = [lambda i=i: op("v", lambda: v.tensor_copy(T.exo[:, i::16], sb[:, 0:CAP]), [sv], [exk[i]]) for i in range(NO, 16)]
+        scatter(CAP, idops, T.ido, T.wo, T.ho, T.dd, T.ofo, copies, exk, T.exo, "o")
+
+    def take(name):
+        k, shifts = MSG[name]
+        n = len(shifts) * CAP
+        ld, lk = T["land" + name], ["land" + name] + (["lown"] if 0 in shifts else [])
+        e16, ids, idf = T["ex" + name], T["ids" + name], T["idf" + name]
+        exk = ["ex%s_%d" % (name, i) for i in range(16)]
+        na = NA if k == 1 else 0
+        for i in range(na):
+            op("a", lambda: a.activation(e16[:, i::16], ld[:, :, 0:CAP], F.Copy), lk, [exk[i]])
+        idops = [
+            lambda: op("v", lambda: v.tensor_tensor(idf[:], ld[:, :, CAP:CAP + 2], T["base" + name][:], A.add), lk + ["base" + name], ["idf" + name]),
+            lambda: op("v", lambda: v.tensor_copy(ids[:], idf[:]), ["idf" + name], ["ids" + name])]
+        copies = [lambda i=i: op("v", lambda: v.tensor_copy(e16[:, i::16], ld[:, :, 0:CAP]), lk, [exk[i]]) for i in range(na, 16)]
+        scatter(n, idops, ids, T["w" + name], T["h" + name], T["d" + name], T["of" + name], copies, exk, e16, name)
+
+    def bases(name):
+        for i, s in enumerate(MSG[name][1]):
+            op("q", lambda: g.iota(T["base" + name][:, i, :], [[0, 2]], V * ((r - s) % N), 0, allow_small_or_imprecise_dtypes=True), [], ["base%s_%d" % (name, i)])
+        lw["base" + name] = ("q", cnt["q"])
+
+    def scan():
+        for c, (lo, hi) in enumerate(PIECES):
+            m = (hi - lo) * P
+            op("v", lambda: v.tensor_tensor_scan(T.so[:, 0:m], T.d0[:, lo * P:hi * P], T.d1[:, lo * P:hi * P], 0.0, A.add, A.max),
+               zk + ["d0_%d_%d" % (c, j) for j in range(8)], ["so"])
+            op("v", lambda: v.tensor_tensor(T.a0[:, lo:hi], T.so[:, P - 1:m:P], T.pt[:, lo:hi], A.add), ["so", "pt"], ["a0_%d" % c])
+            op("v", lambda: v.tensor_tensor(T.xe[:, lo:hi], T.a0[:, lo:hi], T.pt[:, V + lo:V + hi], A.max), ["a0_%d" % c, "mm"], ["x"])
+        op("v", lambda: v.tensor_tensor(T.mx[:], T.xe[:, 0:V], T.la[:, 0:V], A.max), ["x", "la"], ["mx"])
+        op("p", lambda: t.matmul(T.ps[:, 0:V], T.bm[:], T.la[:, 0:V], True, False), ["bm", "la"], ["ps"])
+        op("p", lambda: t.matmul(T.ps[:, 0:V], T.bm[:], T.xe[:, 0:V], False, False), ["bm", "x"], ["ps"])
+        op("p", lambda: t.matmul(T.ps[:, 0:V], T.b2[:], T.mx[:], False, True), ["b2", "mx"], ["ps"])
+
+    a0k = ["a0_%d" % c for c in range(len(PIECES))]
+
+    def after(k):
+        lo, hi = (k + 1) * V, (k + 2) * V
+        op("v", lambda: v.tensor_copy(T.la[:, 0:L].indirect(T.raw[:, 0:2]), T["sb%d" % k][:, 0:CAP]), ["raw0", "raw1", "sbv%d" % k], ["la"])
+        op("v", lambda: v.tensor_scalar(T.drs[:, lo:hi], T.dri[:, lo:hi], Z, None, A.add), ["dri1"], ["drs%d" % (k + 1)])
+        op("v", lambda: v.tensor_scalar(T.a0[:], T.xe[:, 0:V], float(DEC), None, A.subtract), ["x"], a0k)
+        op("v", lambda: v.tensor_copy(T.xe[:, V:L], T.la[:, 0:CAP]), ["la"], ["xp"])
+        op("v", lambda: v.tensor_tensor(T.pt[:, V:2 * V], T.a0[:], T.drs[:, lo:hi], A.max), a0k + ["drs%d" % (k + 1), "pt"], ["mm"])
+
+    op("v", lambda: v.tensor_scalar(T.a0[:], T.x0i[:], DEC - Z, None, A.subtract), ["x0i"], a0k)
+    op("v", lambda: v.tensor_scalar(T.drs[:, 0:V], T.dri[:, 0:V], Z, None, A.add), ["dri0"], ["drs0"])
+    op("v", lambda: v.tensor_tensor(T.xe[:, 0:V], T.a0[:], T.drs[:, 0:V], A.max), a0k + ["drs0"], ["x"])
+    op("p", lambda: t.matmul(T.ps[:, 0:V], T.b1[:], T.xe[:, 0:V], True, True), ["b1", "x"], ["ps"])
+    op("v", lambda: v.tensor_scalar(T.th0[:], T.thi[:], 16 * Z, None, A.add), ["thi"], ["th0"])
+    op("v", lambda: v.tensor_copy(T.thf[:], T.thi[:]), ["thi"], ["thf"])
+    choose(0, False)
+    send("m0")
+    select(2)
+    select(0)
+    for name in MSG:
+        bases(name)
+    dma("s", T.landm0[:, 7, :], T.sb0[:], ["sbv0", "sbi0"], ["lown"], "down")
+    need("s", {"sentm0": cnt["sentm0"]})
+    zdma((8, 9, 10))
+    zact((3, 4))
+
+    op("v", lambda: v.tensor_copy(T.rc[:, :, 8], T.ci[:, 0, :]), ["ci0"], ["rc0_7", "rc1_7"])
+    for c, (lo, hi) in enumerate(((0, MP), (MP, V))):
+        for q in range(7):
+            op("v", lambda: v.tensor_copy(T.rc[:, lo:hi, 1 + q], T.ci[:, 7 - q, lo:hi]), ["ci%d" % (7 - q)], ["rc%d_%d" % (c, q)])
+    op("p", lambda: t.matmul(T.pt[:, 0:V], T.ns[:], T.rc[:, :, 8], True, True), ["ns", "rc0_7", "rc1_7"], ["pt"])
+    n = 0
+    for c, (lo, hi) in enumerate(PIECES):
+        rk = ["rc0"] + ["rc%d_%d" % (min(c, 1), q) for q in range(8)]
+        for j in range(8):
+            pd, pk = T["pd%d" % (n % 2)], "pd%d" % (n % 2)
+            n += 1
+            for s in range(lo, hi, 32):
+                for u in range(2):
+                    b = 15 - j - 8 * u
+                    out = pd[:, 16 * (s - lo) + u:16 * (s - lo) + 512:2]
+                    op("p", lambda: t.matmul(out, T.sel[:, 128 * b:128 * b + 128], T.rc[:, s:s + 32, 1:9], True, b < 15), ["sel%d" % (b // 4)] + rk, [pk])
+                    if b == 15:
+                        op("p", lambda: t.matmul(out, T.ns[:], T.rc[:, s:s + 32, 0:8], False, True), ["ns"] + rk, [pk])
+            op("a", lambda: a.activation(T.d0[:, lo * P + j:hi * P:8], pd[:, 0:16 * (hi - lo)], F.Copy), [pk], ["d0_%d_%d" % (c, j)])
+    op("a", lambda: a.activation(T.b2[:], T.b1[:], F.Copy, scale=2.0), ["b1"], ["b2"])
+    op("a", lambda: a.activation(T.bm[:], T.b1[:], F.Copy, scale=-1.0), ["b1"], ["bm"])
+    after(0)
+    op("v", lambda: v.memset(zu(11, 5), Z), [], ["z%d" % u for u in range(11, 16)])
+    take("m0")
+    scan()
+    choose(1, False)
+    send("m1")
+    after(1)
+    own(1)
+    take("m1")
+    op("a", lambda: a.activation(T.l32[:], T.la[:], F.Identity, bias=-Z), ["la"], ["l32"])
+    scan()
+    choose(2, True)
+    op("a", lambda: a.activation(T.x32[:], T.xe[:, 0:V], F.Identity, bias=-Z), ["x"], ["x32"])
+    dma("s", T.yx[:], T.x32[:], ["x32"], [], "dyx")
+    op("v", lambda: v.tensor_copy(T.l32[:, 0:L].indirect(T.raw[:, 0:2]), T.v32[:]), ["raw0", "raw1", "v32"], ["l32"])
+    dma("s", T.yl[:], T.l32[:, 0:V], ["l32"], [], "dyl")
+    need("s", dict(cnt))

@@ -1,46 +1,40 @@
+import math
 from concourse.bass import DstId, RemoteDMATransfer
 from concourse.mybir import AluOpType as A, AxisListType, ActivationFunctionType as F
 
 N, V, CAP, RO, DEC = 8, 256, 32, 3, 24
-P = 128
-W = V * P
-Z = -255.0
-U = W // 16
-PIECES = ((0, 96), (96, 192), (192, 256))
-MP = 96
+W = V * 128
+H = W // 2
+G = 16
 L = V + CAP
-NA = 9
-NO = 8
-MSG = {"m0": (0, (1, 2, 3, 4, 5, 6, 7, 0)), "m1": (1, (1, 2, 3, 4, 5, 6, 7))}
-X, K, C, Q, B = 16511.5, 128.0 / 32769.0, 12582912.0, 32769.0, 16383.248046875
-F32, BF, I32, U16 = "float32", "bfloat16", "int32", "uint16"
+S = N * CAP
+MID = 1912.0
+LAM = math.log(2.0) / 40.0
+C = 12582912.0
+X, K, Q = 16639.5, 64.0 / 32769.0, 32769.0
+B = 63.25 + 64.0 * X - 32.0 * Q
+CHUNKS = ((0, 32), (32, 64), (64, 128), (128, 192), (192, 256))
+PIECES = ((0, 112), (112, 224), (224, 256))
+U = 1024
+F32, BF, I32, U16, F16 = "float32", "bfloat16", "int32", "uint16", "float16"
 
 SCRATCH = {}
 for _n, _m, _t in (
-        ("x0i", V, I32), ("dri", RO * V, I32), ("thi", 1, I32), ("thf", 1, F32), ("th0", 1, F32), ("drs", RO * V, BF),
-        ("fani", 2048, I32), ("sel", 2048, BF), ("ones", 512, BF), ("nones", 128, BF), ("ns", 128, BF), ("bt", 128, BF),
-        ("b1", 128, BF), ("b2", 128, BF), ("bm", 128, BF), ("d0", W, BF), ("d1", W, BF), ("so", MP * P, BF),
+        ("x0i", V, I32), ("dri", RO * V, I32), ("thi", 1, I32), ("thf", 1, F32), ("fani", 2048, I32), ("ci", 2048, I32), ("cn", 2048, BF),
+        ("ones", 128, BF), ("bt", 128, BF), ("b1", 128, BF), ("b2", 128, BF), ("bm", 128, BF), ("idb", 128, BF), ("idh", 128, F16),
+        ("wsb", V, F32), ("dn", W, BF), ("zt", W, BF), ("so", H, BF), ("cc", 1, F32), ("fi", 1, F32), ("fl", 1, BF),
         ("pi", 2, I32), ("jc", 1, F32), ("jb", 1, F32), ("c33", L, BF), ("xe", L, BF), ("la", L, BF), ("a0", V, BF), ("mx", V, BF),
-        ("chg", L, BF), ("cum", L, BF), ("le", L, BF), ("sg", L, BF), ("acc", 1, F32), ("cnt", 2, F32), ("tt2", 2, F32), ("raw", 2, U16),
-        ("sb0", CAP + 2, BF), ("sb1", CAP + 2, BF), ("wo", CAP, F32), ("ho", CAP, F32), ("dd", CAP, F32), ("ido", 2, U16),
-        ("ofo", CAP, U16), ("exo", CAP * 16, BF), ("l32", L, F32), ("x32", V, F32), ("v32", CAP, F32)):
+        ("ln", V, F32), ("rr", V, F32), ("chg", L, BF), ("cum", L, BF), ("le", L + 1, BF), ("sg", L, BF), ("acc", 2, F32), ("cb", 2, F32),
+        ("tt2", 2, F32), ("raw", 2, U16), ("sb0", CAP + 2, F16), ("sb1", CAP + 2, F16), ("ids", S // 16, U16), ("w", S, F32), ("dd", S, F32),
+        ("es", S, U16), ("of", S, U16), ("gm", 16 * S, BF), ("en", 16 * S, BF), ("l32", L, F32), ("x32", V, F32), ("v32", CAP, F32)):
     SCRATCH[_n] = ("sbuf", [128, _m], _t)
-SCRATCH["ci"] = ("sbuf", [128, 8, V], I32)
-SCRATCH["rc"] = ("sbuf", [128, V, 9], BF)
-for _n, _m in (("pd0", 1536), ("pd1", 1536), ("ps", 512), ("pt", 512)):
+for _n in ("land0", "land1"):
+    SCRATCH[_n] = ("sbuf", [128, N - 1, CAP + 2], F16)
+for _n, _m in (("pc0", 1024), ("pc1", 1024), ("ps", 512), ("pt", 512), ("pv", 512)):
     SCRATCH[_n] = ("psum", [128, _m], F32)
-for _n, (_k, _s) in MSG.items():
-    _m = len(_s)
-    SCRATCH["land" + _n] = ("sbuf", [128, _m, CAP + 2], BF)
-    for _b in ("base", "idf"):
-        SCRATCH[_b + _n] = ("sbuf", [128, _m, 2], F32)
-    SCRATCH["ids" + _n] = ("sbuf", [128, 2 * _m], U16)
-    for _b in ("w", "h", "d"):
-        SCRATCH[_b + _n] = ("sbuf", [128, _m * CAP], F32)
-    SCRATCH["of" + _n] = ("sbuf", [128, _m * CAP], U16)
-    SCRATCH["ex" + _n] = ("sbuf", [128, _m * CAP * 16], BF)
-DMAS = ["dx", "dd0", "dth", "dfan", "dd1", "down", "dyx", "dyl"] + ["dc%d" % q for q in range(8)] + ["dz%d" % u for u in range(16)]
-SEMAPHORES = ["v", "a", "p", "q"] + ["arr" + n for n in MSG] + ["sent" + n for n in MSG] + DMAS
+DMAS = (["dx", "dd0", "dth", "dfan", "dd1", "dyx", "dyl", "dc"] + ["dz%d" % u for u in range(9)]
+        + ["d%s%d" % (n, c) for n in ("dn", "zt") for c in range(16)])
+SEMAPHORES = ["v", "a", "p", "q", "arr0", "arr1", "sent0", "sent1"] + DMAS
 
 
 def rank_program(g, core, T, topo):
@@ -82,213 +76,241 @@ def rank_program(g, core, T, topo):
             lr[k] = {}
 
     v, a, t = g.vector, g.scalar, g.tensor
-    zk = ["z%d" % u for u in range(16)]
+    NU = W // U
 
-    def zu(u, n=1):
-        return T.d1[:, u * U:(u + n) * U]
+    def uk(tab, u=0, n=NU):
+        return ["%s%d" % (tab, i) for i in range(u, u + n)]
 
     def dma(e, out, in_, rd, wr, sem):
         op(e, lambda: eng[e].dma_start(out, in_), rd, wr, sem, 16)
 
-    def zdma(us):
-        for u in us:
-            dma("s", zu(u), zu(0), ["z0"], ["z%d" % u], "dz%d" % u)
+    def fill(e, tab, u, n, sem=None):
+        m = min(n, 2)
+        out, src, sk = T[tab][:, u * U:(u + n) * U], T[tab][:, W - 2 * U:W - (2 - m) * U], uk(tab, NU - 2, m)
+        if e == "q":
+            op("q", lambda: g.iota(out, [[0, n * U // 16], [17, 16]], -255, 0, allow_small_or_imprecise_dtypes=True), [], uk(tab, u, n))
+        elif e == "v":
+            op("v", lambda: v.tensor_copy(out, src), sk, uk(tab, u, n))
+        elif e == "a":
+            op("a", lambda: a.activation(out, src, F.Copy), sk, uk(tab, u, n))
+        else:
+            dma("s", out, src, sk, uk(tab, u, n), sem)
 
-    def zact(us):
-        for u in us:
-            op("a", lambda: a.activation(zu(u), zu(0), F.Copy), ["z0"], ["z%d" % u])
+    def costs(tab, blocks):
+        for c in blocks:
+            dma("s", T[tab][c::16, 2 * U * c:2 * U * (c + 1)], T.cn[c::16, :], ["cn"], uk(tab, 2 * c, 2), "d%s%d" % (tab, c))
 
     dma("s", T.x0i[:], T.x0[:], [], ["x0i"], "dx")
-    dma("s", T.dri[:, 0:V], T.drv[:, 0:V], [], ["dri0"], "dd0")
+    dma("a", T.dri[:, 0:V], T.drv[:, 0:V], [], ["dri0"], "dd0")
     dma("s", T.thi[:], T.th[:], [], ["thi"], "dth")
-    for q in (0, 7, 6, 5, 4, 3, 2, 1):
-        dma("s", T.ci[:, q, :], T.cost[:, 16 * V * q:16 * V * (q + 1)], [], ["ci%d" % q], "dc%d" % q)
-    dma("s", T.dri[:, V:3 * V], T.drv[:, V:3 * V], [], ["dri1"], "dd1")
+    dma("s", T.ci[:], T.cost[:], [], ["ci"], "dc")
     dma("s", T.fani[:], T.fan[:], [], ["fan"], "dfan")
 
+    z0 = W - 2 * U
+    op("q", lambda: g.iota(T.dn[:, z0:z0 + U // 2], [[0, U // 32], [17, 16]], -255, 0, allow_small_or_imprecise_dtypes=True), [], ["seed"])
     op("v", lambda: v.memset(T.ones[:], 1.0), [], ["ones"])
-    op("q", lambda: g.affine_select(T.bt[:], T.ones[:, 0:128], [[-16, 8], [0, 16]], A.is_ge, 0.0, 0, 1), ["ones"], ["bt"])
-    op("q", lambda: g.affine_select(T.b1[:], T.bt[:], [[16, 8], [0, 16]], A.is_ge, 0.0, 15, -1), ["bt"], ["b1"])
     op("q", lambda: g.iota(T.pi[:, 0:1], [[0, 1]], 0, 1), [], ["pi0"])
-
-    def select(k):
-        op("q", lambda: g.affine_select(T.sel[:, 512 * k:512 * k + 512], T.ones[:], [[-1, 4], [-16, 8], [0, 16]], A.is_equal, 0.0, -4 * k, 1),
-           ["ones"], ["sel%d" % k])
-        m = 3 if k == 3 else 4
-        s = T.sel[:, 512 * k:512 * k + 128 * m]
-        op("q", lambda: g.affine_select(s, s, [[-1, m], [-16, 8], [0, 16]], A.not_equal, -1.0, -4 * k - 1, 1), ["sel%d" % k], ["sel%d" % k])
-
-    op("v", lambda: v.memset(zu(0), Z), [], ["z0"])
-    op("v", lambda: v.memset(T.nones[:], -1.0), [], ["nones"])
-    op("q", lambda: g.affine_select(T.ns[:], T.nones[:], [[-16, 8], [0, 16]], A.is_equal, 0.0, 0, 1), ["nones"], ["ns"])
-    select(3)
-    select(1)
+    op("q", lambda: g.affine_select(T.bt[:], T.ones[:], [[-16, 8], [0, 16]], A.is_ge, 0.0, 0, 1), ["ones"], ["bt"])
+    op("q", lambda: g.affine_select(T.b1[:], T.bt[:], [[16, 8], [0, 16]], A.is_ge, 0.0, 15, -1), ["bt"], ["b1"])
+    op("q", lambda: g.affine_select(T.idb[:], T.ones[:], [[-1, 128]], A.is_equal, 0.0, 0, 1), ["ones"], ["idb"])
+    op("v", lambda: v.memset(T.fi[:], -2200.0), [], ["fi"])
+    op("a", lambda: a.activation(T.fl[:], T.fi[:], F.Exp, scale=LAM), ["fi"], ["fl"])
     op("v", lambda: v.memset(T.c33[:], float(CAP + 1)), [], ["c33"])
-    op("v", lambda: v.memset(T.xe[:, V:L], Z), [], ["xp"])
+    op("v", lambda: v.memset(T.xe[:, V:L], 0.0), [], ["xp"])
+    op("v", lambda: v.memset(T.la[:], 0.0), [], ["la"])
+    op("v", lambda: v.memset(T.le[:, L:L + 1], -float(L)), [], ["lel"])
+    op("v", lambda: v.memset(T.cc[:], C), [], ["cc"])
+    op("v", lambda: v.tensor_copy(T.dn[:, z0 + U // 2:z0 + U], T.dn[:, z0:z0 + U // 2]), ["seed"], uk("dn", NU - 2, 1))
     op("v", lambda: v.tensor_scalar(T.pi[:, 1:2], T.pi[:, 0:1], 15, None, A.bitwise_and), ["pi0"], ["pi1"])
+    fill("v", "dn", NU - 1, 1)
     op("v", lambda: v.tensor_scalar(T.jc[:], T.pi[:, 1:2], 16.0, None, A.add), ["pi1"], ["jc"])
     op("v", lambda: v.tensor_scalar(T.jb[:], T.pi[:, 1:2], 0.5, None, A.add), ["pi1"], ["jb"])
-    op("v", lambda: v.memset(T.rc[:, :, 0], 1024.0), [], ["rc0"])
-    op("v", lambda: v.memset(T.la[:], Z), [], ["la"])
-    zact((1, 2))
-    zdma((5, 6, 7))
+    fill("v", "dn", 0, 1)
+    fill("a", "dn", 1, 1)
+    fill("a", "dn", 2, 2)
+    fill("q", "dn", 4, 1)
 
-    def choose(k, last):
-        th, tk = (T.th0, "th0") if k == 0 else (T.thf, "thf")
-        op("v", lambda: v.tensor_scalar(T.chg[:, 0:V], T.ps[:, 0:V], th[:, 0:1], None, A.is_ge), ["ps", tk], ["chg"])
-        op("v", lambda: v.tensor_scalar(T.chg[:, V:L], T.ps[:, 0:CAP], th[:, 0:1], None, A.is_lt), ["ps", tk], ["chp"])
-        op("v", lambda: v.tensor_tensor_scan(T.cum[:], T.chg[:], T.c33[:], 0.0, A.add, A.min), ["chg", "chp", "c33"], ["cum"])
-        op("a", lambda: a.activation(T.sg[:], T.cum[:], F.Sign, bias=T.jb[:, 0:1], scale=-1.0, accum_out=T.acc[:]), ["cum", "jb"], ["sg", "acc"])
-        op("v", lambda: v.tensor_scalar(T.le[:], T.cum[:], T.jc[:, 0:1], None, A.is_le), ["cum", "jc"], ["le"])
-        op("v", lambda: v.tensor_reduce(T.cnt[:, 1:2], T.le[:], AxisListType.X, A.add), ["le"], ["cnt1"])
-        op("v", lambda: v.tensor_scalar(T.raw[:, 0:1], T.acc[:], 0.5, L / 2.0, A.mult, A.add), ["acc"], ["raw0"])
-        op("v", lambda: v.tensor_copy(T.raw[:, 1:2], T.cnt[:, 1:2]), ["cnt1"], ["raw1"])
-        if last:
-            op("v", lambda: v.tensor_scalar(T.v32[:], T.xe[:, 0:L].indirect(T.raw[:, 0:2]), -Z, None, A.add), ["x", "xp", "raw0", "raw1"], ["v32"])
+    def pk(name):
+        return ["%s%d" % (name, c) for c in range(len(PIECES))]
+
+    def choose(k):
+        op("v", lambda: v.tensor_scalar(T.chg[:, V:L], T.chg[:, 0:CAP], -1.0, 1.0, A.mult, A.add), ["chg0"], ["chp"])
+        op("v", lambda: v.tensor_tensor_scan(T.cum[:], T.chg[:], T.c33[:], 0.0, A.add, A.min), pk("chg") + ["chp", "c33"], ["cum"])
+        op("a", lambda: a.activation(T.sg[:], T.cum[:], F.Sign, bias=T.jb[:, 0:1], scale=-1.0, accum_out=T.acc[:, 0:1]), ["cum", "jb"], ["sg", "acc0"])
+        op("v", lambda: v.tensor_scalar(T.le[:, 0:L], T.cum[:], T.jc[:, 0:1], 2.0, A.is_le, A.mult), ["cum", "jc"], ["le"])
+        op("v", lambda: v.tensor_reduce(T.acc[:, 1:2], T.le[:], AxisListType.X, A.add), ["le", "lel"], ["acc1"])
+        acc = ["acc0", "acc1"]
+        op("v", lambda: v.tensor_scalar(T.raw[:], T.acc[:], 0.5, L / 2.0, A.mult, A.add), acc, ["raw"])
+        if k == RO - 1:
+            op("v", lambda: v.tensor_copy(T.v32[:], T.xe[:, 0:L].indirect(T.raw[:, 0:2])), pk("x") + ["xp", "raw"], ["v32"])
             return
         sb = T["sb%d" % k]
-        op("v", lambda: v.tensor_scalar(T.cnt[:, 0:1], T.acc[:], 0.5, L / 2.0, A.mult, A.add), ["acc"], ["cnt0"])
-        op("v", lambda: v.tensor_copy(sb[:, 0:CAP], T.xe[:, 0:L].indirect(T.raw[:, 0:2])), ["x", "xp", "raw0", "raw1"], ["sbv%d" % k])
-        op("v", lambda: v.tensor_scalar(T.tt2[:], T.cnt[:], float(V), -float(V), A.is_ge, A.mult), ["cnt0", "cnt1"], ["tt2"])
-        op("v", lambda: v.tensor_tensor(sb[:, CAP:CAP + 2], T.cnt[:], T.tt2[:], A.add), ["cnt0", "cnt1", "tt2"], ["sbi%d" % k])
+        op("v", lambda: v.tensor_scalar(T.tt2[:], T.acc[:], float(2 * V - L), -float(V), A.is_ge, A.mult), acc, ["tt2"])
+        op("v", lambda: v.tensor_scalar(T.cb[:], T.acc[:], 0.5, L / 2.0 + V * r, A.mult, A.add), acc, ["cb"])
+        op("v", lambda: v.tensor_copy(sb[:, 0:CAP], T.xe[:, 0:L].indirect(T.raw[:, 0:2])), pk("x") + ["xp", "raw"], ["sbv%d" % k])
+        op("v", lambda: v.tensor_tensor(sb[:, CAP:CAP + 2], T.cb[:], T.tt2[:], A.add), ["cb", "tt2"], ["sbi%d" % k])
 
-    def send(name):
-        k, shifts = MSG[name]
-        sb = T["sb%d" % k]
+    def send(k):
         need("q", {"v": max(lw["sbv%d" % k][1], lw["sbi%d" % k][1])})
         ids, dsts, n = [], [], 0
-        for i, s in enumerate(shifts):
-            if s == 0:
-                continue
+        for s in range(1, N):
             rid, pid, _ = topo.addr(T.cores[(r + s) % N])
             ids.append(DstId(rid=rid, pnc=pid))
-            dsts.append(T["land" + name][:, i, :])
+            dsts.append(T["land%d" % k][:, s - 1, :])
             n += len(topo.engines(T.cores[(r - s) % N], core))
         peer = T.cores[(r + 1) % N]
-        g.remote_dma_fused([RemoteDMATransfer(dst_ids=ids, dma_engine_mask=topo.mask(core, peer), remote_sem=T.sem["arr" + name], srcs=[sb[:]], dsts=dsts)],
-                           local_sem=T.sem["sent" + name])
-        cnt["sent" + name] = len(topo.engines(core, peer))
-        cnt["arr" + name] = n
-        lw["land" + name] = ("arr" + name, n)
+        g.remote_dma_fused([RemoteDMATransfer(dst_ids=ids, dma_engine_mask=topo.mask(core, peer), remote_sem=T.sem["arr%d" % k],
+                                              srcs=[T["sb%d" % k][:]], dsts=dsts)], local_sem=T.sem["sent%d" % k])
+        cnt["sent%d" % k] = len(topo.engines(core, peer))
+        cnt["arr%d" % k] = n
+        lw["land%d" % k] = ("arr%d" % k, n)
 
-    def scatter(n, idops, ids, w, h, d, of, copies, exk, e16, tag):
-        steps = idops + [
-            lambda: op("v", lambda: v.tensor_scalar(w[:], T.fani[:, 0:2048].indirect(ids[:, 0:n // 16]), X, K, A.subtract, A.mult), ["fan", "ids" + tag], ["w" + tag]),
-            lambda: op("v", lambda: v.tensor_scalar(h[:], w[:], C, C, A.add, A.subtract), ["w" + tag], ["h" + tag]),
-            lambda: op("v", lambda: v.tensor_tensor(d[:], w[:], h[:], A.subtract), ["w" + tag, "h" + tag], ["d" + tag]),
-            lambda: op("v", lambda: v.tensor_scalar(of[:], d[:], Q, B, A.mult, A.add), ["d" + tag], ["of" + tag])]
-        done = 0
-        for i, step in enumerate(steps):
-            step()
-            upto = len(copies) * (i + 1) // len(steps)
-            for c in copies[done:upto]:
-                c()
-            done = upto
-        op("v", lambda: v.tensor_copy(T.d1[:, 0:W].indirect(of[:, 0:n]), e16[:]), ["of" + tag] + exk, zk)
+    def index(k, own):
+        lo, hi, tag = (0, CAP, "o") if own else (CAP, S, "m")
+        src, sk = (T["sb%d" % k][:, CAP:CAP + 2], "sbi%d" % k) if own else (T["land%d" % k][:, :, CAP:CAP + 2], "land%d" % k)
+        ids, w, h, d = T.ids[:, lo // 16:hi // 16], T.w[:, lo:hi], T.pv[:, lo:hi], T.dd[:, lo:hi]
 
-    def own(k):
-        sb, sv = T["sb%d" % k], "sbv%d" % k
-        exk = ["exo%d" % i for i in range(16)]
-        for i in range(NO):
-            op("a", lambda: a.activation(T.exo[:, i::16], sb[:, 0:CAP], F.Copy), [sv], [exk[i]])
-        idops = [lambda: op("v", lambda: v.tensor_scalar(T.ido[:], sb[:, CAP:CAP + 2], float(V * r), None, A.add), ["sbi%d" % k], ["idso"])]
-        copies = [lambda i=i: op("v", lambda: v.tensor_copy(T.exo[:, i::16], sb[:, 0:CAP]), [sv], [exk[i]]) for i in range(NO, 16)]
-        scatter(CAP, idops, T.ido, T.wo, T.ho, T.dd, T.ofo, copies, exk, T.exo, "o")
+        def slots():
+            op("v", lambda: v.tensor_copy(ids, src), [sk], ["ids" + tag])
+            op("v", lambda: v.tensor_copy(T.es[:, lo:hi], T.fani[:, 0:2048].indirect(ids)), ["fan", "ids" + tag], ["es" + tag])
 
-    def take(name):
-        k, shifts = MSG[name]
-        n = len(shifts) * CAP
-        ld, lk = T["land" + name], ["land" + name] + (["lown"] if 0 in shifts else [])
-        e16, ids, idf = T["ex" + name], T["ids" + name], T["idf" + name]
-        exk = ["ex%s_%d" % (name, i) for i in range(16)]
-        na = NA if k == 1 else 0
-        for i in range(na):
-            op("a", lambda: a.activation(e16[:, i::16], ld[:, :, 0:CAP], F.Copy), lk, [exk[i]])
-        idops = [
-            lambda: op("v", lambda: v.tensor_tensor(idf[:], ld[:, :, CAP:CAP + 2], T["base" + name][:], A.add), lk + ["base" + name], ["idf" + name]),
-            lambda: op("v", lambda: v.tensor_copy(ids[:], idf[:]), ["idf" + name], ["ids" + name])]
-        copies = [lambda i=i: op("v", lambda: v.tensor_copy(e16[:, i::16], ld[:, :, 0:CAP]), lk, [exk[i]]) for i in range(na, 16)]
-        scatter(n, idops, ids, T["w" + name], T["h" + name], T["d" + name], T["of" + name], copies, exk, e16, name)
+        def columns():
+            op("v", lambda: v.tensor_scalar(w, T.es[:, lo:hi], X, K, A.subtract, A.mult), ["es" + tag], ["w" + tag])
+            op("v", lambda: v.tensor_scalar(h, w, C, C, A.add, A.subtract), ["w" + tag], ["h" + tag])
+            op("v", lambda: v.tensor_tensor(d, w, h, A.subtract), ["w" + tag, "h" + tag], ["d" + tag])
+            op("v", lambda: v.tensor_scalar(T.of[:, lo:hi], d, Q, B, A.mult, A.add), ["d" + tag], ["of" + tag])
 
-    def bases(name):
-        for i, s in enumerate(MSG[name][1]):
-            op("q", lambda: g.iota(T["base" + name][:, i, :], [[0, 2]], V * ((r - s) % N), 0, allow_small_or_imprecise_dtypes=True), [], ["base%s_%d" % (name, i)])
-        lw["base" + name] = ("q", cnt["q"])
+        return slots, columns
+
+    turn = [0]
+
+    def stages(k, c):
+        lo, hi = CHUNKS[c]
+        tag, tab = "o" if lo == 0 else "m", ("dn", "zt")[k]
+        nb = (hi - lo) // CAP
+        e0, e1, key, per = 16 * lo, 16 * hi, str(lo), 16 // nb
+        val, vk = (T["sb%d" % k][:, 0:CAP], "sbv%d" % k) if lo == 0 else (T["land%d" % k][:, lo // CAP - 1:hi // CAP - 1, 0:CAP], "land%d" % k)
+        win = T[tab][:, 0:W].indirect(T.es[:, lo:hi])
+
+        def code():
+            name = "pc%d" % (turn[0] % 2)
+            turn[0] += 1
+            pc = T[name]
+            for b in range(nb):
+                for j in range(per):
+                    op("p", lambda: t.matmul(pc[:, 512 * b + j:512 * b + 512:per], T.idh[:], val, j == 0, False), ["idh", vk], [name + str(b)])
+            for b in range(nb):
+                op("p", lambda: t.matmul(pc[:, 512 * b:512 * b + 512], T.b1[:], T.gm[:, e0 + b:e1:nb], False, True), ["b1", "gm" + key], [name + str(b)])
+            for b in range(nb):
+                op("a", lambda: a.activation(T.en[:, e0 + b:e1:nb], pc[:, 512 * b:512 * b + 512], F.Exp, bias=MID * LAM, scale=LAM),
+                   [name + str(b)], ["en%s_%d" % (key, b)])
+
+        return {
+            "v": lambda: op("v", lambda: v.tensor_copy(T.gm[:, e0:e1], win), uk(tab) + ["es" + tag], ["gm" + key]),
+            "a": lambda: op("a", lambda: a.activation(T.gm[:, e0:e1], win, F.Copy), uk(tab) + ["es" + tag], ["gm" + key]),
+            "e": code,
+            "x": lambda: op("v", lambda: v.tensor_copy(T.dn[:, 0:W].indirect(T.of[:, lo:hi]), T.en[:, e0:e1]),
+                            ["of" + tag] + ["en%s_%d" % (key, b) for b in range(nb)], uk("dn"))}
+
+    def work(k, order):
+        for x in order:
+            if isinstance(x, str):
+                stages(k, int(x[1]))[x[0]]()
+            else:
+                x()
+
+    def sums(c):
+        lo, hi = PIECES[c]
+        op("v", lambda: v.tensor_tensor(T.mx[:, lo:hi], T.xe[:, lo:hi], T.la[:, lo:hi], A.max), ["x%d" % c, "la"], ["mx%d" % c])
+        op("p", lambda: t.matmul(T.ps[:, lo:hi], T.bm[:], T.la[:, lo:hi], True, False), ["bm", "la"], ["ps"])
+        op("p", lambda: t.matmul(T.ps[:, lo:hi], T.bm[:], T.xe[:, lo:hi], False, False), ["bm", "x%d" % c], ["ps"])
+        op("p", lambda: t.matmul(T.ps[:, lo:hi], T.b2[:], T.mx[:, lo:hi], False, True), ["b2", "mx%d" % c], ["ps"])
+
+    def changed(c):
+        lo, hi = PIECES[c]
+        op("v", lambda: v.tensor_scalar(T.chg[:, lo:hi], T.ps[:, lo:hi], T.thf[:, 0:1], None, A.is_ge), ["ps", "thf"], ["chg%d" % c])
 
     def scan():
-        for c, (lo, hi) in enumerate(PIECES):
-            m = (hi - lo) * P
-            op("v", lambda: v.tensor_tensor_scan(T.so[:, 0:m], T.d0[:, lo * P:hi * P], T.d1[:, lo * P:hi * P], 0.0, A.add, A.max),
-               zk + ["d0_%d_%d" % (c, j) for j in range(8)], ["so"])
-            op("v", lambda: v.tensor_tensor(T.a0[:, lo:hi], T.so[:, P - 1:m:P], T.pt[:, lo:hi], A.add), ["so", "pt"], ["a0_%d" % c])
-            op("v", lambda: v.tensor_tensor(T.xe[:, lo:hi], T.a0[:, lo:hi], T.pt[:, V + lo:V + hi], A.max), ["a0_%d" % c, "mm"], ["x"])
-        op("v", lambda: v.tensor_tensor(T.mx[:], T.xe[:, 0:V], T.la[:, 0:V], A.max), ["x", "la"], ["mx"])
-        op("p", lambda: t.matmul(T.ps[:, 0:V], T.bm[:], T.la[:, 0:V], True, False), ["bm", "la"], ["ps"])
-        op("p", lambda: t.matmul(T.ps[:, 0:V], T.bm[:], T.xe[:, 0:V], False, False), ["bm", "x"], ["ps"])
-        op("p", lambda: t.matmul(T.ps[:, 0:V], T.b2[:], T.mx[:], False, True), ["b2", "mx"], ["ps"])
+        def run(u):
+            lo, hi = 64 * G * u, 64 * G * (u + 1)
+            op("v", lambda: v.tensor_tensor_scan(T.so[:, lo:hi], T.dn[:, lo:hi], T.dn[:, H + lo:H + hi], T.fl[:, 0:1], A.max, A.max),
+               uk("dn") + ["fl"], ["so%d" % u])
 
-    a0k = ["a0_%d" % c for c in range(len(PIECES))]
+        def read(c):
+            lo, hi = PIECES[c]
+            op("a", lambda: a.activation(T.ln[:, lo:hi], T.so[:, 64 * lo + 63:64 * hi:64], F.Ln), ["so%d" % u for u in range(lo // G, hi // G)], ["ln%d" % c])
+            op("a", lambda: a.activation(T.rr[:, lo:hi], T.ln[:, lo:hi], F.Identity, bias=T.cc[:, 0:1], scale=1.0 / LAM), ["ln%d" % c, "cc"], ["rr%d" % c])
+
+        def level(c):
+            lo, hi = PIECES[c]
+            op("v", lambda: v.tensor_tensor(T.a0[:, lo:hi], T.rr[:, lo:hi], T.pt[:, lo:hi], A.subtract), ["rr%d" % c, "tc"], ["a0%d" % c])
+            op("v", lambda: v.tensor_tensor(T.xe[:, lo:hi], T.a0[:, lo:hi], T.pt[:, V + lo:V + hi], A.max), ["a0%d" % c, "mm"], ["x%d" % c])
+            sums(c)
+
+        todo = {}
+        for c, (lo, hi) in enumerate(PIECES):
+            last = hi // G - 1
+            todo.setdefault(last, []).append((read, c))
+            todo.setdefault(last + (5 if c == 0 else 2), []).append((level, c))
+            todo.setdefault(last + (6 if c == 0 else 3), []).append((changed, c))
+        for u in range(max(todo) + 1):
+            if u < V // G:
+                run(u)
+            for f, c in todo.get(u, []):
+                f(c)
 
     def after(k):
         lo, hi = (k + 1) * V, (k + 2) * V
-        op("v", lambda: v.tensor_copy(T.la[:, 0:L].indirect(T.raw[:, 0:2]), T["sb%d" % k][:, 0:CAP]), ["raw0", "raw1", "sbv%d" % k], ["la"])
-        op("v", lambda: v.tensor_scalar(T.drs[:, lo:hi], T.dri[:, lo:hi], Z, None, A.add), ["dri1"], ["drs%d" % (k + 1)])
-        op("v", lambda: v.tensor_scalar(T.a0[:], T.xe[:, 0:V], float(DEC), None, A.subtract), ["x"], a0k)
+        op("v", lambda: v.tensor_copy(T.la[:, 0:L].indirect(T.raw[:, 0:2]), T["sb%d" % k][:, 0:CAP]), ["raw", "sbv%d" % k], ["la"])
+        op("v", lambda: v.tensor_scalar(T.pt[:, V:2 * V], T.xe[:, 0:V], float(DEC), None, A.subtract), pk("x"), ["mm"])
         op("v", lambda: v.tensor_copy(T.xe[:, V:L], T.la[:, 0:CAP]), ["la"], ["xp"])
-        op("v", lambda: v.tensor_tensor(T.pt[:, V:2 * V], T.a0[:], T.drs[:, lo:hi], A.max), a0k + ["drs%d" % (k + 1), "pt"], ["mm"])
+        op("v", lambda: v.tensor_tensor(T.pt[:, V:2 * V], T.pt[:, V:2 * V], T.dri[:, lo:hi], A.max), ["mm", "dri1"], ["mm"])
 
-    op("v", lambda: v.tensor_scalar(T.a0[:], T.x0i[:], DEC - Z, None, A.subtract), ["x0i"], a0k)
-    op("v", lambda: v.tensor_scalar(T.drs[:, 0:V], T.dri[:, 0:V], Z, None, A.add), ["dri0"], ["drs0"])
-    op("v", lambda: v.tensor_tensor(T.xe[:, 0:V], T.a0[:], T.drs[:, 0:V], A.max), a0k + ["drs0"], ["x"])
-    op("p", lambda: t.matmul(T.ps[:, 0:V], T.b1[:], T.xe[:, 0:V], True, True), ["b1", "x"], ["ps"])
-    op("v", lambda: v.tensor_scalar(T.th0[:], T.thi[:], 16 * Z, None, A.add), ["thi"], ["th0"])
+    op("v", lambda: v.tensor_scalar(T.pv[:, 0:V], T.x0i[:], float(DEC), None, A.subtract), ["x0i"], ["ho", "hm"])
+    op("v", lambda: v.tensor_tensor(T.xe[:, 0:V], T.pv[:, 0:V], T.dri[:, 0:V], A.max), ["ho", "dri0"], pk("x"))
+    op("p", lambda: t.matmul(T.ps[:, 0:V], T.b1[:], T.xe[:, 0:V], True, True), ["b1"] + pk("x"), ["ps"])
     op("v", lambda: v.tensor_copy(T.thf[:], T.thi[:]), ["thi"], ["thf"])
-    choose(0, False)
-    send("m0")
-    select(2)
-    select(0)
-    for name in MSG:
-        bases(name)
-    dma("s", T.landm0[:, 7, :], T.sb0[:], ["sbv0", "sbi0"], ["lown"], "down")
-    need("s", {"sentm0": cnt["sentm0"]})
-    zdma((8, 9, 10))
-    zact((3, 4))
-
-    op("v", lambda: v.tensor_copy(T.rc[:, :, 8], T.ci[:, 0, :]), ["ci0"], ["rc0_7", "rc1_7"])
-    for c, (lo, hi) in enumerate(((0, MP), (MP, V))):
-        for q in range(7):
-            op("v", lambda: v.tensor_copy(T.rc[:, lo:hi, 1 + q], T.ci[:, 7 - q, lo:hi]), ["ci%d" % (7 - q)], ["rc%d_%d" % (c, q)])
-    op("p", lambda: t.matmul(T.pt[:, 0:V], T.ns[:], T.rc[:, :, 8], True, True), ["ns", "rc0_7", "rc1_7"], ["pt"])
-    n = 0
-    for c, (lo, hi) in enumerate(PIECES):
-        rk = ["rc0"] + ["rc%d_%d" % (min(c, 1), q) for q in range(8)]
-        for j in range(8):
-            pd, pk = T["pd%d" % (n % 2)], "pd%d" % (n % 2)
-            n += 1
-            for s in range(lo, hi, 32):
-                for u in range(2):
-                    b = 15 - j - 8 * u
-                    out = pd[:, 16 * (s - lo) + u:16 * (s - lo) + 512:2]
-                    op("p", lambda: t.matmul(out, T.sel[:, 128 * b:128 * b + 128], T.rc[:, s:s + 32, 1:9], True, b < 15), ["sel%d" % (b // 4)] + rk, [pk])
-                    if b == 15:
-                        op("p", lambda: t.matmul(out, T.ns[:], T.rc[:, s:s + 32, 0:8], False, True), ["ns"] + rk, [pk])
-            op("a", lambda: a.activation(T.d0[:, lo * P + j:hi * P:8], pd[:, 0:16 * (hi - lo)], F.Copy), [pk], ["d0_%d_%d" % (c, j)])
+    fill("v", "dn", 5, 1)
+    op("v", lambda: v.tensor_scalar(T.chg[:, 0:V], T.ps[:, 0:V], T.thf[:, 0:1], None, A.is_ge), ["ps", "thf"], pk("chg"))
+    choose(0)
+    send(0)
+    fill("q", "dn", 6, 3)
+    for u in (10, 12, 14):
+        fill("a", "dn", u, 2)
+    fill("a", "dn", 9, 1)
+    fill("a", "dn", 29, 1)
+    fill("s", "dn", 26, 2, "dz8")
+    fill("v", "dn", 16, 2)
+    op("v", lambda: v.tensor_scalar(T.cn[:], T.ci[:], -1.0, None, A.mult), ["ci"], ["cn"])
+    for u in range(18, 26, 2):
+        fill("v", "dn", u, 2)
+    fill("v", "dn", 28, 1)
+    op("v", lambda: v.tensor_copy(T.idh[:], T.idb[:]), ["idb"], ["idh"])
+    costs("dn", (0, 1, 2, 8, 5, 9, 10, 3, 6, 11, 7, 4, 13, 12, 14, 15))
+    dma("s", T.dri[:, V:3 * V], T.drv[:, V:3 * V], [], ["dri1"], "dd1")
+    op("q", lambda: g.iota(T.wsb[:], [[0, V // G], [255, G]], int(MID) - 255 * (G - 1), 0, allow_small_or_imprecise_dtypes=True), [], ["wsb"])
+    fill("q", "zt", NU - 2, 2)
+    fill("q", "zt", 0, 6)
+    for i in range(8):
+        fill("s", "zt", 6 + 2 * i, 2, "dz%d" % i)
     op("a", lambda: a.activation(T.b2[:], T.b1[:], F.Copy, scale=2.0), ["b1"], ["b2"])
     op("a", lambda: a.activation(T.bm[:], T.b1[:], F.Copy, scale=-1.0), ["b1"], ["bm"])
-    after(0)
-    op("v", lambda: v.memset(zu(11, 5), Z), [], ["z%d" % u for u in range(11, 16)])
-    take("m0")
+    op("a", lambda: a.activation(T.pt[:, 0:V], T.wsb[:], F.Identity, bias=T.cc[:, 0:1]), ["wsb", "cc"], ["tc", "mm"])
+    mine, others = index(0, True), index(0, False)
+    work(0, [mine[0], others[0], mine[1], others[1], "a0", "v3", "a1", "e0", "v4", "a2", "e1", lambda: after(0), "e2", "x0", "e3", "x1", "e4", "x2", "x3", "x4"])
+    for u in range(22, NU - 2, 2):
+        fill("a", "zt", u, 2)
+    costs("zt", (3, 4, 5, 6, 11, 7, 0, 12, 1, 8, 13, 2, 9, 14, 10, 15))
     scan()
-    choose(1, False)
-    send("m1")
-    after(1)
-    own(1)
-    take("m1")
-    op("a", lambda: a.activation(T.l32[:], T.la[:], F.Identity, bias=-Z), ["la"], ["l32"])
+    choose(1)
+    send(1)
+    mine, others = index(1, True), index(1, False)
+    work(1, [mine[0], "v0", "e0", mine[1], lambda: after(1), others[0], "a2", "v1", others[1], "e1", "x0", "a3", "e2", "x1", "a4", "e3", "x2", "e4", "x3", "x4"])
+    op("a", lambda: a.activation(T.l32[:], T.la[:], F.Copy), ["la"], ["l32"])
     scan()
-    choose(2, True)
-    op("a", lambda: a.activation(T.x32[:], T.xe[:, 0:V], F.Identity, bias=-Z), ["x"], ["x32"])
+    op("a", lambda: a.activation(T.x32[:], T.xe[:, 0:V], F.Copy), pk("x"), ["x32"])
     dma("s", T.yx[:], T.x32[:], ["x32"], [], "dyx")
-    op("v", lambda: v.tensor_copy(T.l32[:, 0:L].indirect(T.raw[:, 0:2]), T.v32[:]), ["raw0", "raw1", "v32"], ["l32"])
+    choose(2)
+    op("v", lambda: v.tensor_copy(T.l32[:, 0:L].indirect(T.raw[:, 0:2]), T.v32[:]), ["raw", "v32"], ["l32"])
     dma("s", T.yl[:], T.l32[:, 0:V], ["l32"], [], "dyl")
     need("s", dict(cnt))

@@ -13,28 +13,27 @@ LAM = math.log(2.0) / 40.0
 C = 12582912.0
 X, K, Q = 16639.5, 64.0 / 32769.0, 32769.0
 B = 63.25 + 64.0 * X - 32.0 * Q
-CHUNKS = ((0, 32), (32, 64), (64, 128), (128, 192), (192, 256))
-PIECES = ((0, 112), (112, 224), (224, 256))
-U = 1024
+PIECES = ((0, 96), (96, 208), (208, 256))
+PARTS = (((0, 1), (1, 8)), ((0, 1), (1, 4), (4, 8)))
+U = 512
 F32, BF, I32, U16, F16 = "float32", "bfloat16", "int32", "uint16", "float16"
 
 SCRATCH = {}
 for _n, _m, _t in (
-        ("x0i", V, I32), ("dri", RO * V, I32), ("thi", 1, I32), ("thf", 1, F32), ("fani", 2048, I32), ("ci", 2048, I32), ("cn", 2048, BF),
-        ("ones", 128, BF), ("bt", 128, BF), ("b1", 128, BF), ("b2", 128, BF), ("bm", 128, BF), ("idb", 128, BF), ("idh", 128, F16),
-        ("wsb", V, F32), ("dn", W, BF), ("zt", W, BF), ("so", H, BF), ("cc", 1, F32), ("fi", 1, F32), ("fl", 1, BF),
-        ("pi", 2, I32), ("jc", 1, F32), ("jb", 1, F32), ("c33", L, BF), ("xe", L, BF), ("la", L, BF), ("a0", V, BF), ("mx", V, BF),
+        ("x0i", V, I32), ("dri", RO * V, I32), ("thi", 1, I32), ("thf", 1, F32), ("thn", 1, F32), ("thp", 1, F32), ("fani", 2048, I32),
+        ("ci", 2048, I32), ("cn", 2048, BF), ("ones", L, BF), ("bt", 128, BF), ("b1", 128, BF), ("b2", 128, BF), ("bm", 128, BF),
+        ("idb", 128, BF), ("idh", 128, F16), ("wsb", V, F32), ("dn", W, BF), ("zt", W, BF), ("so", H, BF), ("cc", 1, F32), ("fi", 1, F32),
+        ("fl", 1, BF), ("pi", 2, I32), ("jc", 1, BF), ("jb", 1, F32), ("xe", L, BF), ("la", L, BF), ("a0", V, BF), ("mx", V, BF),
         ("ln", V, F32), ("rr", V, F32), ("chg", L, BF), ("cum", L, BF), ("le", L + 1, BF), ("sg", L, BF), ("acc", 2, F32), ("cb", 2, F32),
         ("tt2", 2, F32), ("raw", 2, U16), ("sb0", CAP + 2, F16), ("sb1", CAP + 2, F16), ("ids", S // 16, U16), ("w", S, F32), ("dd", S, F32),
         ("es", S, U16), ("of", S, U16), ("gm", 16 * S, BF), ("en", 16 * S, BF), ("l32", L, F32), ("x32", V, F32), ("v32", CAP, F32)):
     SCRATCH[_n] = ("sbuf", [128, _m], _t)
 for _n in ("land0", "land1"):
     SCRATCH[_n] = ("sbuf", [128, N - 1, CAP + 2], F16)
-for _n, _m in (("pc0", 1024), ("pc1", 1024), ("ps", 512), ("pt", 512), ("pv", 512)):
+for _n, _m in (("pc0", 1024), ("pc1", 1024), ("ps", 512), ("pt", 512), ("pv", 512), ("pa", 512)):
     SCRATCH[_n] = ("psum", [128, _m], F32)
-DMAS = (["dx", "dd0", "dth", "dfan", "dd1", "dyx", "dyl", "dc"] + ["dz%d" % u for u in range(9)]
-        + ["d%s%d" % (n, c) for n in ("dn", "zt") for c in range(16)])
-SEMAPHORES = ["v", "a", "p", "q", "arr0", "arr1", "sent0", "sent1"] + DMAS
+DMAS = ["dx", "dd0", "dth", "dfan", "dd1", "dyx", "dyl", "dc", "ddn", "dzt"] + ["dz%d" % u for u in range(9)]
+SEMAPHORES = ["v", "a", "p", "q"] + ["%s%d_%d" % (n, k, p) for n in ("arr", "sent") for k in range(2) for p in range(1, len(PARTS[k]))] + DMAS
 
 
 def rank_program(g, core, T, topo):
@@ -52,7 +51,6 @@ def rank_program(g, core, T, topo):
 
     def op(e, fn, rd, wr, sem=None, inc=1):
         deps = {}
-        own = e if sem is None else None
         for k in rd:
             if k in lw:
                 s, c = lw[k]
@@ -62,8 +60,7 @@ def rank_program(g, core, T, topo):
                 s, c = lw[k]
                 deps[s] = max(deps.get(s, 0), c)
             for s, c in lr.get(k, {}).items():
-                if s != own:
-                    deps[s] = max(deps.get(s, 0), c)
+                deps[s] = max(deps.get(s, 0), c)
         need(e, deps)
         ins = fn()
         s = sem or e
@@ -81,61 +78,36 @@ def rank_program(g, core, T, topo):
     def uk(tab, u=0, n=NU):
         return ["%s%d" % (tab, i) for i in range(u, u + n)]
 
+    def pk(name):
+        return ["%s%d" % (name, c) for c in range(len(PIECES))]
+
+    def sk(name, lo, hi):
+        return ["%s_%d" % (name, i) for i in range(lo // 16, (hi + 15) // 16)]
+
     def dma(e, out, in_, rd, wr, sem):
         op(e, lambda: eng[e].dma_start(out, in_), rd, wr, sem, 16)
 
     def fill(e, tab, u, n, sem=None):
-        m = min(n, 2)
-        out, src, sk = T[tab][:, u * U:(u + n) * U], T[tab][:, W - 2 * U:W - (2 - m) * U], uk(tab, NU - 2, m)
+        m = min(n, 4)
+        out, src, ks = T[tab][:, u * U:(u + n) * U], T[tab][:, W - 4 * U:W - (4 - m) * U], uk(tab, NU - 4, m)
         if e == "q":
             op("q", lambda: g.iota(out, [[0, n * U // 16], [17, 16]], -255, 0, allow_small_or_imprecise_dtypes=True), [], uk(tab, u, n))
         elif e == "v":
-            op("v", lambda: v.tensor_copy(out, src), sk, uk(tab, u, n))
+            op("v", lambda: v.tensor_copy(out, src), ks, uk(tab, u, n))
         elif e == "a":
-            op("a", lambda: a.activation(out, src, F.Copy), sk, uk(tab, u, n))
+            op("a", lambda: a.activation(out, src, F.Copy), ks, uk(tab, u, n))
         else:
-            dma("s", out, src, sk, uk(tab, u, n), sem)
+            dma("s", out, src, ks, uk(tab, u, n), sem)
 
     def costs(tab, blocks):
         for c in blocks:
-            dma("s", T[tab][c::16, 2 * U * c:2 * U * (c + 1)], T.cn[c::16, :], ["cn"], uk(tab, 2 * c, 2), "d%s%d" % (tab, c))
-
-    dma("s", T.x0i[:], T.x0[:], [], ["x0i"], "dx")
-    dma("a", T.dri[:, 0:V], T.drv[:, 0:V], [], ["dri0"], "dd0")
-    dma("s", T.thi[:], T.th[:], [], ["thi"], "dth")
-    dma("s", T.ci[:], T.cost[:], [], ["ci"], "dc")
-    dma("s", T.fani[:], T.fan[:], [], ["fan"], "dfan")
-
-    z0 = W - 2 * U
-    op("q", lambda: g.iota(T.dn[:, z0:z0 + U // 2], [[0, U // 32], [17, 16]], -255, 0, allow_small_or_imprecise_dtypes=True), [], ["seed"])
-    op("v", lambda: v.memset(T.ones[:], 1.0), [], ["ones"])
-    op("q", lambda: g.iota(T.pi[:, 0:1], [[0, 1]], 0, 1), [], ["pi0"])
-    op("q", lambda: g.affine_select(T.bt[:], T.ones[:], [[-16, 8], [0, 16]], A.is_ge, 0.0, 0, 1), ["ones"], ["bt"])
-    op("q", lambda: g.affine_select(T.b1[:], T.bt[:], [[16, 8], [0, 16]], A.is_ge, 0.0, 15, -1), ["bt"], ["b1"])
-    op("q", lambda: g.affine_select(T.idb[:], T.ones[:], [[-1, 128]], A.is_equal, 0.0, 0, 1), ["ones"], ["idb"])
-    op("v", lambda: v.memset(T.fi[:], -2200.0), [], ["fi"])
-    op("a", lambda: a.activation(T.fl[:], T.fi[:], F.Exp, scale=LAM), ["fi"], ["fl"])
-    op("v", lambda: v.memset(T.c33[:], float(CAP + 1)), [], ["c33"])
-    op("v", lambda: v.memset(T.xe[:, V:L], 0.0), [], ["xp"])
-    op("v", lambda: v.memset(T.la[:], 0.0), [], ["la"])
-    op("v", lambda: v.memset(T.le[:, L:L + 1], -float(L)), [], ["lel"])
-    op("v", lambda: v.memset(T.cc[:], C), [], ["cc"])
-    op("v", lambda: v.tensor_copy(T.dn[:, z0 + U // 2:z0 + U], T.dn[:, z0:z0 + U // 2]), ["seed"], uk("dn", NU - 2, 1))
-    op("v", lambda: v.tensor_scalar(T.pi[:, 1:2], T.pi[:, 0:1], 15, None, A.bitwise_and), ["pi0"], ["pi1"])
-    fill("v", "dn", NU - 1, 1)
-    op("v", lambda: v.tensor_scalar(T.jc[:], T.pi[:, 1:2], 16.0, None, A.add), ["pi1"], ["jc"])
-    op("v", lambda: v.tensor_scalar(T.jb[:], T.pi[:, 1:2], 0.5, None, A.add), ["pi1"], ["jb"])
-    fill("v", "dn", 0, 1)
-    fill("a", "dn", 1, 1)
-    fill("a", "dn", 2, 2)
-    fill("q", "dn", 4, 1)
-
-    def pk(name):
-        return ["%s%d" % (name, c) for c in range(len(PIECES))]
+            dma("s", T[tab][c::16, 4 * U * c:4 * U * (c + 1)], T.cn[c::16, :], ["cn"], uk(tab, 4 * c, 4), "d" + tab)
 
     def choose(k):
-        op("v", lambda: v.tensor_scalar(T.chg[:, V:L], T.chg[:, 0:CAP], -1.0, 1.0, A.mult, A.add), ["chg0"], ["chp"])
-        op("v", lambda: v.tensor_tensor_scan(T.cum[:], T.chg[:], T.c33[:], 0.0, A.add, A.min), pk("chg") + ["chp", "c33"], ["cum"])
+        if k == 0:
+            op("v", lambda: v.tensor_tensor_scan(T.cum[:], T.chg[:], T.chg[:], 0.0, A.add, A.max), pk("chg") + ["chp"], ["cum"])
+        else:
+            op("v", lambda: v.tensor_tensor_scan(T.cum[:], T.chg[:], T.ones[:], 0.0, A.add, A.add), pk("chg") + ["chp", "ones"], ["cum"])
         op("a", lambda: a.activation(T.sg[:], T.cum[:], F.Sign, bias=T.jb[:, 0:1], scale=-1.0, accum_out=T.acc[:, 0:1]), ["cum", "jb"], ["sg", "acc0"])
         op("v", lambda: v.tensor_scalar(T.le[:, 0:L], T.cum[:], T.jc[:, 0:1], 2.0, A.is_le, A.mult), ["cum", "jc"], ["le"])
         op("v", lambda: v.tensor_reduce(T.acc[:, 1:2], T.le[:], AxisListType.X, A.add), ["le", "lel"], ["acc1"])
@@ -152,83 +124,94 @@ def rank_program(g, core, T, topo):
 
     def send(k):
         need("q", {"v": max(lw["sbv%d" % k][1], lw["sbi%d" % k][1])})
-        ids, dsts, n = [], [], 0
-        for s in range(1, N):
-            rid, pid, _ = topo.addr(T.cores[(r + s) % N])
-            ids.append(DstId(rid=rid, pnc=pid))
-            dsts.append(T["land%d" % k][:, s - 1, :])
-            n += len(topo.engines(T.cores[(r - s) % N], core))
-        peer = T.cores[(r + 1) % N]
-        g.remote_dma_fused([RemoteDMATransfer(dst_ids=ids, dma_engine_mask=topo.mask(core, peer), remote_sem=T.sem["arr%d" % k],
-                                              srcs=[T["sb%d" % k][:]], dsts=dsts)], local_sem=T.sem["sent%d" % k])
-        cnt["sent%d" % k] = len(topo.engines(core, peer))
-        cnt["arr%d" % k] = n
-        lw["land%d" % k] = ("arr%d" % k, n)
+        for p, (lo, hi) in enumerate(PARTS[k][1:], 1):
+            ids, dsts, n, name = [], [], 0, "%d_%d" % (k, p)
+            for s in range(lo, hi):
+                rid, pid, _ = topo.addr(T.cores[(r + s) % N])
+                ids.append(DstId(rid=rid, pnc=pid))
+                dsts.append(T["land%d" % k][:, s - 1, :])
+                n += len(topo.engines(T.cores[(r - s) % N], core))
+            peer = T.cores[(r + lo) % N]
+            g.remote_dma_fused([RemoteDMATransfer(dst_ids=ids, dma_engine_mask=topo.mask(core, peer), remote_sem=T.sem["arr" + name],
+                                                  srcs=[T["sb%d" % k][:]], dsts=dsts)], local_sem=T.sem["sent" + name])
+            cnt["sent" + name] = len(topo.engines(core, peer))
+            cnt["arr" + name] = n
+            lw["land" + name] = ("arr" + name, n)
 
-    def index(k, own):
-        lo, hi, tag = (0, CAP, "o") if own else (CAP, S, "m")
-        src, sk = (T["sb%d" % k][:, CAP:CAP + 2], "sbi%d" % k) if own else (T["land%d" % k][:, :, CAP:CAP + 2], "land%d" % k)
-        ids, w, h, d = T.ids[:, lo // 16:hi // 16], T.w[:, lo:hi], T.pv[:, lo:hi], T.dd[:, lo:hi]
+    def sources(k, p):
+        s0, s1 = PARTS[k][p]
+        src, key = (T["land%d" % k][:, s0 - 1:s1 - 1, CAP:CAP + 2], "land%d_%d" % (k, p)) if p else (T["sb%d" % k][:, CAP:CAP + 2], "sbi%d" % k)
+        op("v", lambda: v.tensor_copy(T.ids[:, 2 * s0:2 * s1], src), [key], sk("ids", CAP * s0, CAP * s1))
 
-        def slots():
-            op("v", lambda: v.tensor_copy(ids, src), [sk], ["ids" + tag])
-            op("v", lambda: v.tensor_copy(T.es[:, lo:hi], T.fani[:, 0:2048].indirect(ids)), ["fan", "ids" + tag], ["es" + tag])
+    def index(lo, hi):
+        ids, es, w, h, d = T.ids[:, lo // 16:hi // 16], T.es[:, lo:hi], T.w[:, lo:hi], T.pv[:, lo:hi], T.dd[:, lo:hi]
+        return iter([
+            lambda: op("v", lambda: v.tensor_copy(es, T.fani[:, 0:2048].indirect(ids)), ["fan"] + sk("ids", lo, hi), sk("es", lo, hi)),
+            lambda: op("v", lambda: v.tensor_scalar(w, es, X, K, A.subtract, A.mult), sk("es", lo, hi), sk("w", lo, hi)),
+            lambda: op("v", lambda: v.tensor_scalar(h, w, C, C, A.add, A.subtract), sk("w", lo, hi), sk("h", lo, hi)),
+            lambda: op("v", lambda: v.tensor_tensor(d, w, h, A.subtract), sk("w", lo, hi) + sk("h", lo, hi), sk("d", lo, hi)),
+            lambda: op("v", lambda: v.tensor_scalar(T.of[:, lo:hi], d, Q, B, A.mult, A.add), sk("d", lo, hi), sk("of", lo, hi))])
 
-        def columns():
-            op("v", lambda: v.tensor_scalar(w, T.es[:, lo:hi], X, K, A.subtract, A.mult), ["es" + tag], ["w" + tag])
-            op("v", lambda: v.tensor_scalar(h, w, C, C, A.add, A.subtract), ["w" + tag], ["h" + tag])
-            op("v", lambda: v.tensor_tensor(d, w, h, A.subtract), ["w" + tag, "h" + tag], ["d" + tag])
-            op("v", lambda: v.tensor_scalar(T.of[:, lo:hi], d, Q, B, A.mult, A.add), ["d" + tag], ["of" + tag])
-
-        return slots, columns
+    def gather(k, e, lo, hi):
+        tab = ("dn", "zt")[k]
+        out, win = T.gm[:, 16 * lo:16 * hi], T[tab][:, 0:W].indirect(T.es[:, lo:hi])
+        fn = (lambda: v.tensor_copy(out, win)) if e == "v" else (lambda: a.activation(out, win, F.Copy))
+        op(e, fn, uk(tab) + sk("es", lo, hi), sk("gm", lo, hi))
 
     turn = [0]
 
-    def stages(k, c):
-        lo, hi = CHUNKS[c]
-        tag, tab = "o" if lo == 0 else "m", ("dn", "zt")[k]
+    def code(k, lo, hi):
         nb = (hi - lo) // CAP
-        e0, e1, key, per = 16 * lo, 16 * hi, str(lo), 16 // nb
-        val, vk = (T["sb%d" % k][:, 0:CAP], "sbv%d" % k) if lo == 0 else (T["land%d" % k][:, lo // CAP - 1:hi // CAP - 1, 0:CAP], "land%d" % k)
-        win = T[tab][:, 0:W].indirect(T.es[:, lo:hi])
+        e0, e1, per = 16 * lo, 16 * hi, 16 // nb
+        p = [p for p, (s0, s1) in enumerate(PARTS[k]) if s0 * CAP <= lo][-1]
+        val, vk = (T["land%d" % k][:, lo // CAP - 1:hi // CAP - 1, 0:CAP], "land%d_%d" % (k, p)) if lo else (T["sb%d" % k][:, 0:CAP], "sbv%d" % k)
+        name = "pc%d" % (turn[0] % 2)
+        turn[0] += 1
+        pc = T[name]
+        for b in range(nb):
+            for j in range(per):
+                op("p", lambda: t.matmul(pc[:, 512 * b + j:512 * b + 512:per], T.idh[:], val, j == 0, False), ["idh", vk], [name + str(b)])
+        for b in range(nb):
+            op("p", lambda: t.matmul(pc[:, 512 * b:512 * b + 512], T.b1[:], T.gm[:, e0 + b:e1:nb], False, True), ["b1"] + sk("gm", lo, hi), [name + str(b)])
+        for b in range(nb):
+            op("a", lambda: a.activation(T.en[:, e0 + b:e1:nb], pc[:, 512 * b:512 * b + 512], F.Exp, bias=MID * LAM, scale=LAM),
+               [name + str(b)], sk("en%d" % b, lo, hi))
 
-        def code():
-            name = "pc%d" % (turn[0] % 2)
-            turn[0] += 1
-            pc = T[name]
-            for b in range(nb):
-                for j in range(per):
-                    op("p", lambda: t.matmul(pc[:, 512 * b + j:512 * b + 512:per], T.idh[:], val, j == 0, False), ["idh", vk], [name + str(b)])
-            for b in range(nb):
-                op("p", lambda: t.matmul(pc[:, 512 * b:512 * b + 512], T.b1[:], T.gm[:, e0 + b:e1:nb], False, True), ["b1", "gm" + key], [name + str(b)])
-            for b in range(nb):
-                op("a", lambda: a.activation(T.en[:, e0 + b:e1:nb], pc[:, 512 * b:512 * b + 512], F.Exp, bias=MID * LAM, scale=LAM),
-                   [name + str(b)], ["en%s_%d" % (key, b)])
-
-        return {
-            "v": lambda: op("v", lambda: v.tensor_copy(T.gm[:, e0:e1], win), uk(tab) + ["es" + tag], ["gm" + key]),
-            "a": lambda: op("a", lambda: a.activation(T.gm[:, e0:e1], win, F.Copy), uk(tab) + ["es" + tag], ["gm" + key]),
-            "e": code,
-            "x": lambda: op("v", lambda: v.tensor_copy(T.dn[:, 0:W].indirect(T.of[:, lo:hi]), T.en[:, e0:e1]),
-                            ["of" + tag] + ["en%s_%d" % (key, b) for b in range(nb)], uk("dn"))}
+    def scatter(lo, hi):
+        op("v", lambda: v.tensor_copy(T.dn[:, 0:W].indirect(T.of[:, lo:hi]), T.en[:, 16 * lo:16 * hi]),
+           sk("of", lo, hi) + sk("en0", lo, hi) + sk("en1", lo, hi), uk("dn"))
 
     def work(k, order):
-        for x in order:
-            if isinstance(x, str):
-                stages(k, int(x[1]))[x[0]]()
+        rows, nxt = {}, after(k)
+        for x in order.split():
+            if x == "n":
+                next(nxt)()
+            elif x == "c":
+                scalars(k)
+            elif x[0] == "s":
+                sources(k, int(x[1]))
             else:
-                x()
+                lo, hi = [16 * int(m) for m in x[1:].split("-")]
+                if x[0] == "i":
+                    if x not in rows:
+                        rows[x] = index(lo, hi)
+                    next(rows[x])()
+                elif x[0] == "e":
+                    code(k, lo, hi)
+                elif x[0] == "x":
+                    scatter(lo, hi)
+                else:
+                    gather(k, x[0], lo, hi)
 
     def sums(c):
         lo, hi = PIECES[c]
-        op("v", lambda: v.tensor_tensor(T.mx[:, lo:hi], T.xe[:, lo:hi], T.la[:, lo:hi], A.max), ["x%d" % c, "la"], ["mx%d" % c])
+        op("v", lambda: v.tensor_tensor(T.mx[:, lo:hi], T.a0[:, lo:hi], T.pv[:, V + lo:V + hi], A.max), ["a0%d" % c, "ml"], ["mx%d" % c])
         op("p", lambda: t.matmul(T.ps[:, lo:hi], T.bm[:], T.la[:, lo:hi], True, False), ["bm", "la"], ["ps"])
         op("p", lambda: t.matmul(T.ps[:, lo:hi], T.bm[:], T.xe[:, lo:hi], False, False), ["bm", "x%d" % c], ["ps"])
         op("p", lambda: t.matmul(T.ps[:, lo:hi], T.b2[:], T.mx[:, lo:hi], False, True), ["b2", "mx%d" % c], ["ps"])
-
-    def changed(c):
-        lo, hi = PIECES[c]
-        op("v", lambda: v.tensor_scalar(T.chg[:, lo:hi], T.ps[:, lo:hi], T.thf[:, 0:1], None, A.is_ge), ["ps", "thf"], ["chg%d" % c])
+        op("a", lambda: a.activation(T.chg[:, lo:hi], T.ps[:, lo:hi], F.Sign, bias=T.thn[:, 0:1]), ["ps", "thn"], ["chg%d" % c])
+        if c == 0:
+            op("a", lambda: a.activation(T.chg[:, V:L], T.ps[:, 0:CAP], F.Sign, bias=T.thp[:, 0:1], scale=-1.0), ["ps", "thp"], ["chp"])
 
     def scan():
         def run(u):
@@ -244,68 +227,113 @@ def rank_program(g, core, T, topo):
         def level(c):
             lo, hi = PIECES[c]
             op("v", lambda: v.tensor_tensor(T.a0[:, lo:hi], T.rr[:, lo:hi], T.pt[:, lo:hi], A.subtract), ["rr%d" % c, "tc"], ["a0%d" % c])
+
+        def state(c):
+            lo, hi = PIECES[c]
             op("v", lambda: v.tensor_tensor(T.xe[:, lo:hi], T.a0[:, lo:hi], T.pt[:, V + lo:V + hi], A.max), ["a0%d" % c, "mm"], ["x%d" % c])
             sums(c)
 
         todo = {}
         for c, (lo, hi) in enumerate(PIECES):
             last = hi // G - 1
-            todo.setdefault(last, []).append((read, c))
-            todo.setdefault(last + (5 if c == 0 else 2), []).append((level, c))
-            todo.setdefault(last + (6 if c == 0 else 3), []).append((changed, c))
+            todo.setdefault(last, []).insert(0, (read, c))
+            todo.setdefault(last + (5, 2, 1)[c], []).append((level, c))
+            todo.setdefault(last + (6, 3, 1)[c], []).append((state, c))
         for u in range(max(todo) + 1):
             if u < V // G:
                 run(u)
             for f, c in todo.get(u, []):
                 f(c)
 
+    def scalars(k):
+        op("a", lambda: a.activation(T.pa[:, 0:V], T.xe[:, 0:V], F.Identity, bias=-float(DEC)), pk("x"), ["pa"])
+        if k == 0:
+            op("a", lambda: a.activation(T.pt[:, 0:V], T.wsb[:], F.Identity, bias=T.cc[:, 0:1]), ["wsb", "cc"], ["tc", "mm"])
+            op("a", lambda: a.activation(T.b2[:], T.b1[:], F.Copy, scale=2.0), ["b1"], ["b2"])
+            op("a", lambda: a.activation(T.bm[:], T.b1[:], F.Copy, scale=-1.0), ["b1"], ["bm"])
+            op("a", lambda: a.activation(T.thn[:], T.thf[:], F.Identity, bias=0.5, scale=-1.0), ["thf"], ["thn"])
+            op("a", lambda: a.activation(T.thp[:], T.thf[:], F.Identity, bias=-0.5), ["thf"], ["thp"])
+
     def after(k):
         lo, hi = (k + 1) * V, (k + 2) * V
-        op("v", lambda: v.tensor_copy(T.la[:, 0:L].indirect(T.raw[:, 0:2]), T["sb%d" % k][:, 0:CAP]), ["raw", "sbv%d" % k], ["la"])
-        op("v", lambda: v.tensor_scalar(T.pt[:, V:2 * V], T.xe[:, 0:V], float(DEC), None, A.subtract), pk("x"), ["mm"])
-        op("v", lambda: v.tensor_copy(T.xe[:, V:L], T.la[:, 0:CAP]), ["la"], ["xp"])
-        op("v", lambda: v.tensor_tensor(T.pt[:, V:2 * V], T.pt[:, V:2 * V], T.dri[:, lo:hi], A.max), ["mm", "dri1"], ["mm"])
+        return iter([
+            lambda: op("v", lambda: v.tensor_copy(T.la[:, 0:L].indirect(T.raw[:, 0:2]), T["sb%d" % k][:, 0:CAP]), ["raw", "sbv%d" % k], ["la"]),
+            lambda: op("v", lambda: v.tensor_tensor(T.pt[:, V:2 * V], T.pa[:, 0:V], T.dri[:, lo:hi], A.max), ["pa", "dri1", "tc"], ["mm"]),
+            lambda: op("v", lambda: v.tensor_copy(T.xe[:, V:L], T.la[:, 0:CAP]), ["la"], ["xp"]),
+            lambda: op("v", lambda: v.tensor_tensor(T.pv[:, V:2 * V], T.pt[:, V:2 * V], T.la[:, 0:V], A.max), ["mm", "la"], ["ml"])])
 
-    op("v", lambda: v.tensor_scalar(T.pv[:, 0:V], T.x0i[:], float(DEC), None, A.subtract), ["x0i"], ["ho", "hm"])
-    op("v", lambda: v.tensor_tensor(T.xe[:, 0:V], T.pv[:, 0:V], T.dri[:, 0:V], A.max), ["ho", "dri0"], pk("x"))
-    op("p", lambda: t.matmul(T.ps[:, 0:V], T.b1[:], T.xe[:, 0:V], True, True), ["b1"] + pk("x"), ["ps"])
+    dma("s", T.x0i[:], T.x0[:], [], ["x0i"], "dx")
+    dma("a", T.dri[:, 0:V], T.drv[:, 0:V], [], ["dri0"], "dd0")
+    dma("s", T.thi[:], T.th[:], [], ["thi"], "dth")
+    dma("s", T.ci[:], T.cost[:], [], ["ci"], "dc")
+    dma("s", T.fani[:], T.fan[:], [], ["fan"], "dfan")
+
+    z0, s0 = W - 4 * U, U // 4
+    op("q", lambda: g.iota(T.dn[:, z0:z0 + s0], [[0, s0 // 16], [17, 16]], -255, 0, allow_small_or_imprecise_dtypes=True), [], ["seed"])
+    op("v", lambda: v.memset(T.ones[:], 1.0), [], ["ones"])
+    op("q", lambda: g.iota(T.pi[:, 0:1], [[0, 1]], 0, 1), [], ["pi0"])
+    op("q", lambda: g.affine_select(T.bt[:], T.ones[:, 0:128], [[-16, 8], [0, 16]], A.is_ge, 0.0, 0, 1), ["ones"], ["bt"])
+    op("q", lambda: g.affine_select(T.b1[:], T.bt[:], [[16, 8], [0, 16]], A.is_ge, 0.0, 15, -1), ["bt"], ["b1"])
+    op("v", lambda: v.memset(T.la[:], 0.0), [], ["la"])
+    op("v", lambda: v.tensor_copy(T.dn[:, z0 + s0:z0 + 2 * s0], T.dn[:, z0:z0 + s0]), ["seed"], ["seed2"])
+    op("v", lambda: v.memset(T.xe[:, V:L], 0.0), [], ["xp"])
+    op("v", lambda: v.tensor_copy(T.dn[:, z0 + 2 * s0:z0 + U], T.dn[:, z0:z0 + 2 * s0]), ["seed", "seed2"], uk("dn", NU - 4, 1))
+    op("v", lambda: v.tensor_scalar(T.pi[:, 1:2], T.pi[:, 0:1], 15, None, A.bitwise_and), ["pi0"], ["pi1"])
+    fill("v", "dn", NU - 3, 1)
+    op("v", lambda: v.tensor_scalar(T.jc[:], T.pi[:, 1:2], 2.0, 32.0, A.mult, A.add), ["pi1"], ["jc"])
+    fill("v", "dn", NU - 2, 2)
+    op("v", lambda: v.tensor_scalar(T.jb[:], T.pi[:, 1:2], 2.0, 1.0, A.mult, A.add), ["pi1"], ["jb"])
+    op("v", lambda: v.memset(T.le[:, L:L + 1], -float(L)), [], ["lel"])
+    op("v", lambda: v.memset(T.fi[:], -2200.0), [], ["fi"])
+    fill("v", "dn", 0, 2)
+    fill("a", "dn", 2, 1)
+    fill("a", "dn", 3, 2)
+    fill("a", "dn", 5, 4)
+    fill("q", "dn", 9, 2)
+    fill("q", "dn", 11, 1)
+    op("q", lambda: g.affine_select(T.idb[:], T.ones[:, 0:128], [[-1, 128]], A.is_equal, 0.0, 0, 1), ["ones"], ["idb"])
+
+    op("v", lambda: v.tensor_scalar(T.pv[:, 0:V], T.x0i[:], float(DEC), None, A.subtract), ["x0i"], sk("h", 0, S))
     op("v", lambda: v.tensor_copy(T.thf[:], T.thi[:]), ["thi"], ["thf"])
-    fill("v", "dn", 5, 1)
-    op("v", lambda: v.tensor_scalar(T.chg[:, 0:V], T.ps[:, 0:V], T.thf[:, 0:1], None, A.is_ge), ["ps", "thf"], pk("chg"))
+    op("v", lambda: v.tensor_tensor(T.xe[:, 0:V], T.pv[:, 0:V], T.dri[:, 0:V], A.max), sk("h", 0, S) + ["dri0"], pk("x"))
+    op("p", lambda: t.matmul(T.ps[:, 0:V], T.b1[:], T.xe[:, 0:V], True, True), ["b1"] + pk("x"), ["ps"])
+    fill("v", "dn", 12, 2)
+    op("v", lambda: v.tensor_scalar(T.chg[:, 0:V], T.ps[:, 0:V], T.thf[:, 0:1], 2.0, A.is_ge, A.mult), ["ps", "thf"], pk("chg"))
+    op("v", lambda: v.tensor_scalar(T.chg[:, V:L], T.ps[:, 0:CAP], T.thf[:, 0:1], 2.0, A.is_lt, A.mult), ["ps", "thf"], ["chp"])
     choose(0)
     send(0)
-    fill("q", "dn", 6, 3)
-    for u in (10, 12, 14):
-        fill("a", "dn", u, 2)
-    fill("a", "dn", 9, 1)
-    fill("a", "dn", 29, 1)
-    fill("s", "dn", 26, 2, "dz8")
-    fill("v", "dn", 16, 2)
+    fill("q", "dn", 16, 7)
+    fill("s", "dn", 56, 4, "dz8")
+    for u in (24, 28, 32):
+        fill("a", "dn", u, 4)
+    fill("a", "dn", 53, 3)
+    fill("v", "dn", 14, 2)
+    fill("v", "dn", 36, 4)
     op("v", lambda: v.tensor_scalar(T.cn[:], T.ci[:], -1.0, None, A.mult), ["ci"], ["cn"])
-    for u in range(18, 26, 2):
-        fill("v", "dn", u, 2)
-    fill("v", "dn", 28, 1)
+    fill("v", "dn", 23, 1)
+    for u in range(40, 52, 4):
+        fill("v", "dn", u, 4)
+    fill("v", "dn", 52, 1)
     op("v", lambda: v.tensor_copy(T.idh[:], T.idb[:]), ["idb"], ["idh"])
-    costs("dn", (0, 1, 2, 8, 5, 9, 10, 3, 6, 11, 7, 4, 13, 12, 14, 15))
+    op("v", lambda: v.memset(T.cc[:], C), [], ["cc"])
+    costs("dn", (0, 1, 2, 3, 9, 6, 10, 7, 11, 8, 12, 14, 4, 5, 13, 15))
     dma("s", T.dri[:, V:3 * V], T.drv[:, V:3 * V], [], ["dri1"], "dd1")
     op("q", lambda: g.iota(T.wsb[:], [[0, V // G], [255, G]], int(MID) - 255 * (G - 1), 0, allow_small_or_imprecise_dtypes=True), [], ["wsb"])
-    fill("q", "zt", NU - 2, 2)
-    fill("q", "zt", 0, 6)
+    fill("q", "zt", NU - 4, 4)
+    fill("q", "zt", 0, 16)
     for i in range(8):
-        fill("s", "zt", 6 + 2 * i, 2, "dz%d" % i)
-    op("a", lambda: a.activation(T.b2[:], T.b1[:], F.Copy, scale=2.0), ["b1"], ["b2"])
-    op("a", lambda: a.activation(T.bm[:], T.b1[:], F.Copy, scale=-1.0), ["b1"], ["bm"])
-    op("a", lambda: a.activation(T.pt[:, 0:V], T.wsb[:], F.Identity, bias=T.cc[:, 0:1]), ["wsb", "cc"], ["tc", "mm"])
-    mine, others = index(0, True), index(0, False)
-    work(0, [mine[0], others[0], mine[1], others[1], "a0", "v3", "a1", "e0", "v4", "a2", "e1", lambda: after(0), "e2", "x0", "e3", "x1", "e4", "x2", "x3", "x4"])
-    for u in range(22, NU - 2, 2):
-        fill("a", "zt", u, 2)
-    costs("zt", (3, 4, 5, 6, 11, 7, 0, 12, 1, 8, 13, 2, 9, 14, 10, 15))
+        fill("s", "zt", 16 + 4 * i, 4, "dz%d" % i)
+    op("a", lambda: a.activation(T.fl[:], T.fi[:], F.Exp, scale=LAM), ["fi"], ["fl"])
+    work(0, "s0 s1 i0-16 i0-16 i0-16 i0-16 i0-16 a0-2 v7-16 a2-7 e0-2 e2-4 n x0-2 e4-8 x2-4 e8-12 x4-8 e12-16 c n n x8-16 n")
+    for u in range(48, NU - 4, 4):
+        fill("a", "zt", u, 4)
+    costs("zt", (4, 5, 6, 7, 12, 8, 13, 9, 14, 10, 11, 0, 1, 2, 3, 15))
     scan()
     choose(1)
     send(1)
-    mine, others = index(1, True), index(1, False)
-    work(1, [mine[0], "v0", "e0", mine[1], lambda: after(1), others[0], "a2", "v1", others[1], "e1", "x0", "a3", "e2", "x1", "a4", "e3", "x2", "e4", "x3", "x4"])
+    work(1, "c s0 n i0-2 n v0-2 e0-2 i0-2 n i0-2 n i0-2 i0-2 s1 i2-8 a4-8 i2-8 v2-4 i2-8 e2-4 e4-8 x0-2 i2-8 s2 i2-8 i8-16 a8-12 e8-12 "
+            "x2-4 i8-16 i8-16 a12-16 e12-16 x4-8 i8-16 i8-16 x8-12 x12-16")
+    need("s", dict(cnt))
     op("a", lambda: a.activation(T.l32[:], T.la[:], F.Copy), ["la"], ["l32"])
     scan()
     op("a", lambda: a.activation(T.x32[:], T.xe[:, 0:V], F.Copy), pk("x"), ["x32"])

@@ -5,16 +5,18 @@ from concourse.mybir import AluOpType as A, AxisListType, ActivationFunctionType
 N, V, CAP, RO, DEC = 8, 256, 32, 3, 24
 W = V * 128
 H = W // 2
-G = 16
+G = 32
 L = V + CAP
 S = N * CAP
-MID = 1912.0
-LAM = math.log(2.0) / 40.0
+STEPS, LIFT, LOW, DOWN = 71.0, 8811.0, -8161.0, 68
+LAM = math.log(2.0) / STEPS
 C = 12582912.0
 X, K, Q = 16639.5, 64.0 / 32769.0, 32769.0
 B = 63.25 + 64.0 * X - 32.0 * Q
-PIECES = ((0, 96), (96, 208), (208, 256))
+PIECES = ((0, 96), (96, 224), (224, 256))
 PARTS = (((0, 1), (1, 8)), ((0, 1), (1, 4), (4, 8)))
+E = PIECES[-1][0]
+CQ = 768
 U = 512
 F32, BF, I32, U16, F16 = "float32", "bfloat16", "int32", "uint16", "float16"
 
@@ -22,17 +24,19 @@ SCRATCH = {}
 for _n, _m, _t in (
         ("x0i", V, I32), ("dri", RO * V, I32), ("thi", 1, I32), ("thf", 1, F32), ("thn", 1, F32), ("thp", 1, F32), ("fani", 2048, I32),
         ("ci", 2048, I32), ("cn", 2048, BF), ("ones", L, BF), ("bt", 128, BF), ("b1", 128, BF), ("b2", 128, BF), ("bm", 128, BF),
-        ("idb", 128, BF), ("idh", 128, F16), ("wsb", V, F32), ("dn", W, BF), ("zt", W, BF), ("so", H, BF), ("cc", 1, F32), ("fi", 1, F32),
-        ("fl", 1, BF), ("pi", 2, I32), ("jc", 1, BF), ("jb", 1, F32), ("xe", L, BF), ("la", L, BF), ("a0", V, BF), ("mx", V, BF),
+        ("idb", 128, BF), ("nid", 128, BF), ("drb", V, BF), ("r1", V, BF), ("r2", V, BF), ("hh", S, F32), ("id32", 128, F32), ("ntc", V, F32), ("mms", V, BF), ("mls", V, BF),
+        ("idh", 128, F16), ("cm", 1, F32), ("dn", W, BF), ("zt", W, BF), ("so", H, BF), ("cc", 1, F32), ("fi", 1, F32),
+        ("fl", 1, BF), ("pi", 2, I32), ("jc", 1, BF), ("jb", 1, F32), ("jd", 1, F32), ("xe", L, BF), ("la", L, BF), ("a0", V, BF), ("mx", V, BF),
         ("ln", V, F32), ("rr", V, F32), ("chg", L, BF), ("cum", L, BF), ("le", L + 1, BF), ("sg", L, BF), ("acc", 2, F32), ("cb", 2, F32),
         ("tt2", 2, F32), ("raw", 2, U16), ("sb0", CAP + 2, F16), ("sb1", CAP + 2, F16), ("ids", S // 16, U16), ("w", S, F32), ("dd", S, F32),
         ("es", S, U16), ("of", S, U16), ("gm", 16 * S, BF), ("en", 16 * S, BF), ("l32", L, F32), ("x32", V, F32), ("v32", CAP, F32)):
     SCRATCH[_n] = ("sbuf", [128, _m], _t)
+SCRATCH["sd"] = ("sbuf", [128, V // G, G], BF)
 for _n in ("land0", "land1"):
     SCRATCH[_n] = ("sbuf", [128, N - 1, CAP + 2], F16)
 for _n, _m in (("pc0", 1024), ("pc1", 1024), ("ps", 512), ("pt", 512), ("pv", 512), ("pa", 512)):
     SCRATCH[_n] = ("psum", [128, _m], F32)
-DMAS = ["dx", "dd0", "dth", "dfan", "dd1", "dyx", "dyl", "dc", "ddn", "dzt"] + ["dz%d" % u for u in range(9)]
+DMAS = ["dx", "dd0", "dth", "dfan", "dd1", "dyx", "dyl", "dc", "ddn", "dzt"] + ["dz%d" % u for u in range(22)]
 SEMAPHORES = ["v", "a", "p", "q"] + ["%s%d_%d" % (n, k, p) for n in ("arr", "sent") for k in range(2) for p in range(1, len(PARTS[k]))] + DMAS
 
 
@@ -74,6 +78,7 @@ def rank_program(g, core, T, topo):
 
     v, a, t = g.vector, g.scalar, g.tensor
     NU = W // U
+    sdk = ["sd0", "sd1", "sd2"]
 
     def uk(tab, u=0, n=NU):
         return ["%s%d" % (tab, i) for i in range(u, u + n)]
@@ -88,10 +93,9 @@ def rank_program(g, core, T, topo):
         op(e, lambda: eng[e].dma_start(out, in_), rd, wr, sem, 16)
 
     def fill(e, tab, u, n, sem=None):
-        m = min(n, 4)
-        out, src, ks = T[tab][:, u * U:(u + n) * U], T[tab][:, W - 4 * U:W - (4 - m) * U], uk(tab, NU - 4, m)
+        out, src, ks = T[tab][:, u * U:(u + n) * U], T[tab][:, W - 4 * U:W - (4 - n) * U], uk(tab, NU - 4, n)
         if e == "q":
-            op("q", lambda: g.iota(out, [[0, n * U // 16], [17, 16]], -255, 0, allow_small_or_imprecise_dtypes=True), [], uk(tab, u, n))
+            op("q", lambda: g.affine_select(out, src, [[0, n * U]], A.is_ge, 0.0, 0, 0), ks, uk(tab, u, n))
         elif e == "v":
             op("v", lambda: v.tensor_copy(out, src), ks, uk(tab, u, n))
         elif e == "a":
@@ -99,28 +103,39 @@ def rank_program(g, core, T, topo):
         else:
             dma("s", out, src, ks, uk(tab, u, n), sem)
 
-    def costs(tab, blocks):
+    def seed(tab, e):
+        for i in range(2):
+            out = T[tab][:, W - 4 * U + i * V:W - 4 * U + (i + 1) * V]
+            fn = (lambda: v.tensor_copy(out, T.sd[:])) if e == "v" else (lambda: g.affine_select(out, T.sd[:], [[0, V]], A.is_ge, 0.0, 0, 0))
+            op(e, fn, sdk, uk(tab, NU - 4, i))
+
+    def costs(tab, blocks, e="s"):
         for c in blocks:
-            dma("s", T[tab][c::16, 4 * U * c:4 * U * (c + 1)], T.cn[c::16, :], ["cn"], uk(tab, 4 * c, 4), "d" + tab)
+            dma(e, T[tab][c::16, 4 * U * c:4 * U * (c + 1)], T.cn[c::16, :], ["cn0", "cn1"], uk(tab, 4 * c, 4), "d" + tab)
 
     def choose(k):
         if k == 0:
             op("v", lambda: v.tensor_tensor_scan(T.cum[:], T.chg[:], T.chg[:], 0.0, A.add, A.max), pk("chg") + ["chp"], ["cum"])
         else:
-            op("v", lambda: v.tensor_tensor_scan(T.cum[:], T.chg[:], T.ones[:], 0.0, A.add, A.add), pk("chg") + ["chp", "ones"], ["cum"])
+            op("v", lambda: v.tensor_tensor_scan(T.cum[:], T.chg[:], T.ones[:], 0.0, A.add, A.add), pk("chg") + ["chp", "ones", "none"], ["cum"])
         op("a", lambda: a.activation(T.sg[:], T.cum[:], F.Sign, bias=T.jb[:, 0:1], scale=-1.0, accum_out=T.acc[:, 0:1]), ["cum", "jb"], ["sg", "acc0"])
-        op("v", lambda: v.tensor_scalar(T.le[:, 0:L], T.cum[:], T.jc[:, 0:1], 2.0, A.is_le, A.mult), ["cum", "jc"], ["le"])
-        op("v", lambda: v.tensor_reduce(T.acc[:, 1:2], T.le[:], AxisListType.X, A.add), ["le", "lel"], ["acc1"])
+        if k == 0:
+            op("a", lambda: a.activation(T.le[:, 0:L], T.cum[:], F.Sign, bias=T.jd[:, 0:1], scale=-1.0, accum_out=T.acc[:, 1:2]), ["cum", "jd"], ["le", "acc1"])
+            fill("v", "dn", 12, 4)
+        else:
+            op("v", lambda: v.tensor_scalar(T.le[:, 0:L], T.cum[:], T.jc[:, 0:1], 2.0, A.is_le, A.mult), ["cum", "jc"], ["le"])
+            op("v", lambda: v.tensor_reduce(T.acc[:, 1:2], T.le[:], AxisListType.X, A.add), ["le", "lel"], ["acc1"])
         acc = ["acc0", "acc1"]
-        op("v", lambda: v.tensor_scalar(T.raw[:], T.acc[:], 0.5, L / 2.0, A.mult, A.add), acc, ["raw"])
         if k == RO - 1:
+            op("v", lambda: v.tensor_scalar(T.raw[:], T.acc[:], 0.5, L / 2.0, A.mult, A.add), acc, ["raw"])
             op("v", lambda: v.tensor_copy(T.v32[:], T.xe[:, 0:L].indirect(T.raw[:, 0:2])), pk("x") + ["xp", "raw"], ["v32"])
             return
         sb = T["sb%d" % k]
         op("v", lambda: v.tensor_scalar(T.tt2[:], T.acc[:], float(2 * V - L), -float(V), A.is_ge, A.mult), acc, ["tt2"])
         op("v", lambda: v.tensor_scalar(T.cb[:], T.acc[:], 0.5, L / 2.0 + V * r, A.mult, A.add), acc, ["cb"])
-        op("v", lambda: v.tensor_copy(sb[:, 0:CAP], T.xe[:, 0:L].indirect(T.raw[:, 0:2])), pk("x") + ["xp", "raw"], ["sbv%d" % k])
+        op("v", lambda: v.tensor_scalar(T.raw[:], T.acc[:], 0.5, L / 2.0, A.mult, A.add), acc, ["raw"])
         op("v", lambda: v.tensor_tensor(sb[:, CAP:CAP + 2], T.cb[:], T.tt2[:], A.add), ["cb", "tt2"], ["sbi%d" % k])
+        op("v", lambda: v.tensor_copy(sb[:, 0:CAP], T.xe[:, 0:L].indirect(T.raw[:, 0:2])), pk("x") + ["xp", "raw"], ["sbv%d" % k])
 
     def send(k):
         need("q", {"v": max(lw["sbv%d" % k][1], lw["sbi%d" % k][1])})
@@ -143,13 +158,22 @@ def rank_program(g, core, T, topo):
         src, key = (T["land%d" % k][:, s0 - 1:s1 - 1, CAP:CAP + 2], "land%d_%d" % (k, p)) if p else (T["sb%d" % k][:, CAP:CAP + 2], "sbi%d" % k)
         op("v", lambda: v.tensor_copy(T.ids[:, 2 * s0:2 * s1], src), [key], sk("ids", CAP * s0, CAP * s1))
 
-    def index(lo, hi):
-        ids, es, w, h, d = T.ids[:, lo // 16:hi // 16], T.es[:, lo:hi], T.w[:, lo:hi], T.pv[:, lo:hi], T.dd[:, lo:hi]
+    def index(lo, hi, aside):
+        ids, es, w, d = T.ids[:, lo // 16:hi // 16], T.es[:, lo:hi], T.w[:, lo:hi], T.dd[:, lo:hi]
+        h, hk = (T.pa[:, lo:hi], ["pa"]) if aside else (T.pv[:, lo:hi], sk("h", lo, hi))
+
+        def rounded():
+            if aside:
+                op("a", lambda: a.activation(T.hh[:, lo:hi], w, F.Identity, bias=T.cc[:, 0:1]), sk("w", lo, hi) + ["cc"], ["hh"])
+                op("a", lambda: a.activation(h, T.hh[:, lo:hi], F.Identity, bias=-C), ["hh"], hk)
+            else:
+                op("v", lambda: v.tensor_scalar(h, w, C, C, A.add, A.subtract), sk("w", lo, hi), hk)
+
         return iter([
             lambda: op("v", lambda: v.tensor_copy(es, T.fani[:, 0:2048].indirect(ids)), ["fan"] + sk("ids", lo, hi), sk("es", lo, hi)),
             lambda: op("v", lambda: v.tensor_scalar(w, es, X, K, A.subtract, A.mult), sk("es", lo, hi), sk("w", lo, hi)),
-            lambda: op("v", lambda: v.tensor_scalar(h, w, C, C, A.add, A.subtract), sk("w", lo, hi), sk("h", lo, hi)),
-            lambda: op("v", lambda: v.tensor_tensor(d, w, h, A.subtract), sk("w", lo, hi) + sk("h", lo, hi), sk("d", lo, hi)),
+            rounded,
+            lambda: op("v", lambda: v.tensor_tensor(d, w, h, A.subtract), sk("w", lo, hi) + hk, sk("d", lo, hi)),
             lambda: op("v", lambda: v.tensor_scalar(T.of[:, lo:hi], d, Q, B, A.mult, A.add), sk("d", lo, hi), sk("of", lo, hi))])
 
     def gather(k, e, lo, hi):
@@ -165,17 +189,16 @@ def rank_program(g, core, T, topo):
         e0, e1, per = 16 * lo, 16 * hi, 16 // nb
         p = [p for p, (s0, s1) in enumerate(PARTS[k]) if s0 * CAP <= lo][-1]
         val, vk = (T["land%d" % k][:, lo // CAP - 1:hi // CAP - 1, 0:CAP], "land%d_%d" % (k, p)) if lo else (T["sb%d" % k][:, 0:CAP], "sbv%d" % k)
-        name = "pc%d" % (turn[0] % 2)
-        turn[0] += 1
-        pc = T[name]
-        for b in range(nb):
+        banks = [(turn[0] + b) % 4 for b in range(nb)]
+        turn[0] += nb
+        at = [(T["pc%d" % (m // 2)], 512 * (m % 2), "pc%d%d" % (m // 2, m % 2)) for m in banks]
+        for pc, o, key in at:
             for j in range(per):
-                op("p", lambda: t.matmul(pc[:, 512 * b + j:512 * b + 512:per], T.idh[:], val, j == 0, False), ["idh", vk], [name + str(b)])
-        for b in range(nb):
-            op("p", lambda: t.matmul(pc[:, 512 * b:512 * b + 512], T.b1[:], T.gm[:, e0 + b:e1:nb], False, True), ["b1"] + sk("gm", lo, hi), [name + str(b)])
-        for b in range(nb):
-            op("a", lambda: a.activation(T.en[:, e0 + b:e1:nb], pc[:, 512 * b:512 * b + 512], F.Exp, bias=MID * LAM, scale=LAM),
-               [name + str(b)], sk("en%d" % b, lo, hi))
+                op("p", lambda: t.matmul(pc[:, o + j:o + 512:per], T.idh[:], val, j == 0, False), ["idh", vk], [key])
+        for b, (pc, o, key) in enumerate(at):
+            op("p", lambda: t.matmul(pc[:, o:o + 512], T.bm[:], T.gm[:, e0 + b:e1:nb], False, True), ["bm"] + sk("gm", lo, hi), [key])
+        for b, (pc, o, key) in enumerate(at):
+            op("a", lambda: a.activation(T.en[:, e0 + b:e1:nb], pc[:, o:o + 512], F.Exp, bias=LIFT * LAM, scale=LAM), [key], sk("en%d" % b, lo, hi))
 
     def scatter(lo, hi):
         op("v", lambda: v.tensor_copy(T.dn[:, 0:W].indirect(T.of[:, lo:hi]), T.en[:, 16 * lo:16 * hi]),
@@ -188,13 +211,15 @@ def rank_program(g, core, T, topo):
                 next(nxt)()
             elif x == "c":
                 scalars(k)
+            elif x == "d":
+                op("v", lambda: v.tensor_copy(T.idh[:], T.idb[:]), ["idb"], ["idh"])
             elif x[0] == "s":
                 sources(k, int(x[1]))
             else:
                 lo, hi = [16 * int(m) for m in x[1:].split("-")]
-                if x[0] == "i":
+                if x[0] in "ij":
                     if x not in rows:
-                        rows[x] = index(lo, hi)
+                        rows[x] = index(lo, hi, x[0] == "j")
                     next(rows[x])()
                 elif x[0] == "e":
                     code(k, lo, hi)
@@ -205,15 +230,19 @@ def rank_program(g, core, T, topo):
 
     def sums(c):
         lo, hi = PIECES[c]
-        op("v", lambda: v.tensor_tensor(T.mx[:, lo:hi], T.a0[:, lo:hi], T.pv[:, V + lo:V + hi], A.max), ["a0%d" % c, "ml"], ["mx%d" % c])
-        op("p", lambda: t.matmul(T.ps[:, lo:hi], T.bm[:], T.la[:, lo:hi], True, False), ["bm", "la"], ["ps"])
-        op("p", lambda: t.matmul(T.ps[:, lo:hi], T.bm[:], T.xe[:, lo:hi], False, False), ["bm", "x%d" % c], ["ps"])
-        op("p", lambda: t.matmul(T.ps[:, lo:hi], T.b2[:], T.mx[:, lo:hi], False, True), ["b2", "mx%d" % c], ["ps"])
-        op("a", lambda: a.activation(T.chg[:, lo:hi], T.ps[:, lo:hi], F.Sign, bias=T.thn[:, 0:1]), ["ps", "thn"], ["chg%d" % c])
+        key = "ps" if hi <= E else "pa"
+        ps = T[key][:, lo:hi]
+        op("p", lambda: t.matmul(ps, T.bm[:], T.la[:, lo:hi], True, False), ["bm", "la"], [key])
+        op("p", lambda: t.matmul(ps, T.bm[:], T.xe[:, lo:hi], False, False), ["bm", "x%d" % c], [key])
+        op("p", lambda: t.matmul(ps, T.b2[:], T.mx[:, lo:hi], False, True), ["b2", "mx%d" % c], [key])
+        if hi <= E:
+            op("a", lambda: a.activation(T.chg[:, lo:hi], ps, F.Sign, bias=T.thn[:, 0:1]), [key, "thn"], ["chg%d" % c])
+        else:
+            op("v", lambda: v.tensor_scalar(T.chg[:, lo:hi], ps, T.thf[:, 0:1], 2.0, A.is_ge, A.mult), [key, "thf"], ["chg%d" % c])
         if c == 0:
             op("a", lambda: a.activation(T.chg[:, V:L], T.ps[:, 0:CAP], F.Sign, bias=T.thp[:, 0:1], scale=-1.0), ["ps", "thp"], ["chp"])
 
-    def scan():
+    def scan(between=None):
         def run(u):
             lo, hi = 64 * G * u, 64 * G * (u + 1)
             op("v", lambda: v.tensor_tensor_scan(T.so[:, lo:hi], T.dn[:, lo:hi], T.dn[:, H + lo:H + hi], T.fl[:, 0:1], A.max, A.max),
@@ -221,46 +250,82 @@ def rank_program(g, core, T, topo):
 
         def read(c):
             lo, hi = PIECES[c]
-            op("a", lambda: a.activation(T.ln[:, lo:hi], T.so[:, 64 * lo + 63:64 * hi:64], F.Ln), ["so%d" % u for u in range(lo // G, hi // G)], ["ln%d" % c])
-            op("a", lambda: a.activation(T.rr[:, lo:hi], T.ln[:, lo:hi], F.Identity, bias=T.cc[:, 0:1], scale=1.0 / LAM), ["ln%d" % c, "cc"], ["rr%d" % c])
+            op("a", lambda: a.activation(T.ln[:, lo:hi], T.so[:, 64 * lo + 63:64 * hi:64], F.Ln, scale=2.0 ** -DOWN),
+               ["so%d" % u for u in range(lo // G, hi // G)], ["ln%d" % c])
+            if hi <= E:
+                op("a", lambda: a.activation(T.rr[:, lo:hi], T.ln[:, lo:hi], F.Identity, bias=T.cc[:, 0:1], scale=1.0 / LAM), ["ln%d" % c, "cc"], ["rr%d" % c])
 
         def level(c):
             lo, hi = PIECES[c]
-            op("v", lambda: v.tensor_tensor(T.a0[:, lo:hi], T.rr[:, lo:hi], T.pt[:, lo:hi], A.subtract), ["rr%d" % c, "tc"], ["a0%d" % c])
+            if hi <= E:
+                pc, key = T["pc%d" % c][:, 0:hi - lo], "pc%d0" % c
+                op("p", lambda: t.matmul(pc, T.id32[:], T.ntc[:, lo:hi], True, False), ["id32", "ntc"], [key])
+                op("p", lambda: t.matmul(pc, T.id32[:], T.rr[:, lo:hi], False, True), ["id32", "rr%d" % c], [key])
+            else:
+                op("v", lambda: v.tensor_scalar(T.rr[:, lo:hi], T.ln[:, lo:hi], 1.0 / LAM, C, A.mult, A.add), ["ln%d" % c], ["rr%d" % c])
+                op("v", lambda: v.tensor_tensor(T.a0[:, lo:hi], T.rr[:, lo:hi], T.pt[:, lo:hi], A.subtract), ["rr%d" % c, "tc"], ["a0"])
 
         def state(c):
             lo, hi = PIECES[c]
-            op("v", lambda: v.tensor_tensor(T.xe[:, lo:hi], T.a0[:, lo:hi], T.pt[:, V + lo:V + hi], A.max), ["a0%d" % c, "mm"], ["x%d" % c])
+            lv, key, mm, ml = (T["pc%d" % c][:, 0:hi - lo], "pc%d0" % c, T.mms[:, lo:hi], T.mls[:, lo:hi]) if hi <= E else (
+                T.a0[:, lo:hi], "a0", T.pt[:, V + lo:V + hi], T.pv[:, V + lo:V + hi])
+            op("v", lambda: v.tensor_tensor(T.xe[:, lo:hi], lv, mm, A.max), [key, "mm", "mms"], ["x%d" % c])
+            op("v", lambda: v.tensor_tensor(T.mx[:, lo:hi], lv, ml, A.max), [key, "ml", "mls"], ["mx%d" % c])
             sums(c)
 
         todo = {}
         for c, (lo, hi) in enumerate(PIECES):
             last = hi // G - 1
             todo.setdefault(last, []).insert(0, (read, c))
-            todo.setdefault(last + (5, 2, 1)[c], []).append((level, c))
-            todo.setdefault(last + (6, 3, 1)[c], []).append((state, c))
+            todo.setdefault(last + (0, 0, 1)[c], []).append((level, c))
+            todo.setdefault(last + (4, 1, 1)[c], []).append((state, c))
         for u in range(max(todo) + 1):
             if u < V // G:
                 run(u)
             for f, c in todo.get(u, []):
                 f(c)
+                if between and (f, c) == (read, 0):
+                    between()
 
     def scalars(k):
-        op("a", lambda: a.activation(T.pa[:, 0:V], T.xe[:, 0:V], F.Identity, bias=-float(DEC)), pk("x"), ["pa"])
+        if k == 1:
+            op("a", lambda: a.activation(T.pa[:, 0:V], T.xe[:, 0:V], F.Identity, bias=-float(DEC)), pk("x"), ["pa"])
         if k == 0:
-            op("a", lambda: a.activation(T.pt[:, 0:V], T.wsb[:], F.Identity, bias=T.cc[:, 0:1]), ["wsb", "cc"], ["tc", "mm"])
+            op("a", lambda: a.activation(T.cm[:], T.cc[:], F.Identity, bias=LIFT - DOWN * STEPS), ["cc"], ["cm"])
             op("a", lambda: a.activation(T.b2[:], T.b1[:], F.Copy, scale=2.0), ["b1"], ["b2"])
-            op("a", lambda: a.activation(T.bm[:], T.b1[:], F.Copy, scale=-1.0), ["b1"], ["bm"])
+            op("a", lambda: a.activation(T.pt[:, 0:V], T.sd[:], F.Identity, bias=T.cm[:, 0:1], scale=-15.0), sdk + ["cm"], ["tc", "mm"])
+            op("a", lambda: a.activation(T.ntc[:], T.pt[:, 0:V], F.Copy, scale=-1.0), ["tc"], ["ntc"])
+            op("a", lambda: a.activation(T.ones[:, E:V], T.b1[:, 0:V - E], F.Copy, scale=0.0), ["b1", "ones"], ["none"])
+            op("a", lambda: a.activation(T.jc[:], T.jd[:], F.Identity, bias=-1.0), ["jd"], ["jc"])
             op("a", lambda: a.activation(T.thn[:], T.thf[:], F.Identity, bias=0.5, scale=-1.0), ["thf"], ["thn"])
             op("a", lambda: a.activation(T.thp[:], T.thf[:], F.Identity, bias=-0.5), ["thf"], ["thp"])
+
+    def maxima(u):
+        x, la = (T.xe[:, 0:V], pk("x")), (T.la[:, 0:V], ["la"])
+        dr, r1, r2 = (T.drb[:], ["drb"]), (T.r1[:], ["r1"]), (T.r2[:], ["r2"])
+        for i, (plus, minus, out, func, bias, ks) in enumerate((
+                ([x], [dr], T.r1[:], F.Relu, -float(DEC), ["r1"]), ([r1, dr], [], T.pt[:, V + E:2 * V], F.Copy, 0.0, ["mm"]),
+                ([r1, dr], [la], T.r2[:], F.Relu, 0.0, ["r2"]), ([r2, la], [], T.pv[:, V + E:2 * V], F.Copy, 0.0, ["ml"] + sk("h", 0, S)))):
+            terms = [(T.idb, "idb", m) for m in plus] + [(T.nid, "nid", m) for m in minus]
+            for j, (sign, key, (src, rd)) in enumerate(terms):
+                op("p", lambda: t.matmul(T.pa[:, 0:V], sign[:], src, j == 0, j + 1 == len(terms)), [key] + rd, ["pa"])
+            fill("a", "zt", u + i, 1)
+            if i % 2:
+                op("a", lambda: a.activation(T[ks[0] + "s"][:, 0:E], T.pa[:, 0:E], func), ["pa"], [ks[0] + "s"])
+                op("a", lambda: a.activation(out, T.pa[:, E:V], func), ["pa"], ks)
+            else:
+                op("a", lambda: a.activation(out, T.pa[:, 0:V], func, bias=bias), ["pa"], ks)
 
     def after(k):
         lo, hi = (k + 1) * V, (k + 2) * V
         return iter([
             lambda: op("v", lambda: v.tensor_copy(T.la[:, 0:L].indirect(T.raw[:, 0:2]), T["sb%d" % k][:, 0:CAP]), ["raw", "sbv%d" % k], ["la"]),
-            lambda: op("v", lambda: v.tensor_tensor(T.pt[:, V:2 * V], T.pa[:, 0:V], T.dri[:, lo:hi], A.max), ["pa", "dri1", "tc"], ["mm"]),
-            lambda: op("v", lambda: v.tensor_copy(T.xe[:, V:L], T.la[:, 0:CAP]), ["la"], ["xp"]),
-            lambda: op("v", lambda: v.tensor_tensor(T.pv[:, V:2 * V], T.pt[:, V:2 * V], T.la[:, 0:V], A.max), ["mm", "la"], ["ml"])])
+            lambda: op("av"[k], lambda: (v.tensor_copy(T.xe[:, V:L], T.la[:, 0:CAP]) if k else a.activation(T.xe[:, V:L], T.la[:, 0:CAP], F.Copy)),
+                       ["la"], ["xp"]),
+            lambda: op("v", lambda: v.tensor_tensor(T.mms[:, 0:E], T.pa[:, 0:E], T.dri[:, lo:lo + E], A.max), ["pa", "dri1"], ["mms"]),
+            lambda: op("v", lambda: v.tensor_tensor(T.pt[:, V + E:2 * V], T.pa[:, E:V], T.dri[:, lo + E:hi], A.max), ["pa", "dri1", "tc"], ["mm"]),
+            lambda: op("v", lambda: v.tensor_tensor(T.mls[:, 0:E], T.mms[:, 0:E], T.la[:, 0:E], A.max), ["mms", "la"], ["mls"]),
+            lambda: op("v", lambda: v.tensor_tensor(T.pv[:, V + E:2 * V], T.pt[:, V + E:2 * V], T.la[:, E:V], A.max), ["mm", "la"], ["ml"])])
 
     dma("s", T.x0i[:], T.x0[:], [], ["x0i"], "dx")
     dma("a", T.dri[:, 0:V], T.drv[:, 0:V], [], ["dri0"], "dd0")
@@ -268,71 +333,82 @@ def rank_program(g, core, T, topo):
     dma("s", T.ci[:], T.cost[:], [], ["ci"], "dc")
     dma("s", T.fani[:], T.fan[:], [], ["fan"], "dfan")
 
-    z0, s0 = W - 4 * U, U // 4
-    op("q", lambda: g.iota(T.dn[:, z0:z0 + s0], [[0, s0 // 16], [17, 16]], -255, 0, allow_small_or_imprecise_dtypes=True), [], ["seed"])
+    op("q", lambda: g.iota(T.sd[:, :, 16:G], [[0, V // G], [-17, 16]], 255, 0, allow_small_or_imprecise_dtypes=True), [], ["sd2"])
+    op("q", lambda: g.iota(T.sd[:, :, 1:16], [[0, V // G], [-18, 15]], 524, 0, allow_small_or_imprecise_dtypes=True), [], ["sd1"])
+    op("v", lambda: v.memset(T.sd[:, :, 0], 544.0), [], ["sd0"])
     op("v", lambda: v.memset(T.ones[:], 1.0), [], ["ones"])
     op("q", lambda: g.iota(T.pi[:, 0:1], [[0, 1]], 0, 1), [], ["pi0"])
     op("q", lambda: g.affine_select(T.bt[:], T.ones[:, 0:128], [[-16, 8], [0, 16]], A.is_ge, 0.0, 0, 1), ["ones"], ["bt"])
     op("q", lambda: g.affine_select(T.b1[:], T.bt[:], [[16, 8], [0, 16]], A.is_ge, 0.0, 15, -1), ["bt"], ["b1"])
     op("v", lambda: v.memset(T.la[:], 0.0), [], ["la"])
-    op("v", lambda: v.tensor_copy(T.dn[:, z0 + s0:z0 + 2 * s0], T.dn[:, z0:z0 + s0]), ["seed"], ["seed2"])
     op("v", lambda: v.memset(T.xe[:, V:L], 0.0), [], ["xp"])
-    op("v", lambda: v.tensor_copy(T.dn[:, z0 + 2 * s0:z0 + U], T.dn[:, z0:z0 + 2 * s0]), ["seed", "seed2"], uk("dn", NU - 4, 1))
+    op("v", lambda: v.memset(T.le[:, L:L + 1], -float(L)), [], ["lel"])
+    op("v", lambda: v.memset(T.fi[:], LOW + LIFT), [], ["fi"])
+    op("v", lambda: v.memset(T.cc[:], C), [], ["cc"])
+    seed("dn", "v")
     op("v", lambda: v.tensor_scalar(T.pi[:, 1:2], T.pi[:, 0:1], 15, None, A.bitwise_and), ["pi0"], ["pi1"])
     fill("v", "dn", NU - 3, 1)
-    op("v", lambda: v.tensor_scalar(T.jc[:], T.pi[:, 1:2], 2.0, 32.0, A.mult, A.add), ["pi1"], ["jc"])
+    op("v", lambda: v.tensor_scalar(T.jd[:], T.pi[:, 1:2], 2.0, 33.0, A.mult, A.add), ["pi1"], ["jd"])
     fill("v", "dn", NU - 2, 2)
     op("v", lambda: v.tensor_scalar(T.jb[:], T.pi[:, 1:2], 2.0, 1.0, A.mult, A.add), ["pi1"], ["jb"])
-    op("v", lambda: v.memset(T.le[:, L:L + 1], -float(L)), [], ["lel"])
-    op("v", lambda: v.memset(T.fi[:], -2200.0), [], ["fi"])
     fill("v", "dn", 0, 2)
     fill("a", "dn", 2, 1)
     fill("a", "dn", 3, 2)
-    fill("a", "dn", 5, 4)
+    fill("a", "dn", 5, 3)
+    fill("q", "dn", 8, 1)
     fill("q", "dn", 9, 2)
-    fill("q", "dn", 11, 1)
     op("q", lambda: g.affine_select(T.idb[:], T.ones[:, 0:128], [[-1, 128]], A.is_equal, 0.0, 0, 1), ["ones"], ["idb"])
 
     op("v", lambda: v.tensor_scalar(T.pv[:, 0:V], T.x0i[:], float(DEC), None, A.subtract), ["x0i"], sk("h", 0, S))
     op("v", lambda: v.tensor_copy(T.thf[:], T.thi[:]), ["thi"], ["thf"])
     op("v", lambda: v.tensor_tensor(T.xe[:, 0:V], T.pv[:, 0:V], T.dri[:, 0:V], A.max), sk("h", 0, S) + ["dri0"], pk("x"))
     op("p", lambda: t.matmul(T.ps[:, 0:V], T.b1[:], T.xe[:, 0:V], True, True), ["b1"] + pk("x"), ["ps"])
-    fill("v", "dn", 12, 2)
+    fill("v", "dn", 11, 1)
     op("v", lambda: v.tensor_scalar(T.chg[:, 0:V], T.ps[:, 0:V], T.thf[:, 0:1], 2.0, A.is_ge, A.mult), ["ps", "thf"], pk("chg"))
     op("v", lambda: v.tensor_scalar(T.chg[:, V:L], T.ps[:, 0:CAP], T.thf[:, 0:1], 2.0, A.is_lt, A.mult), ["ps", "thf"], ["chp"])
     choose(0)
     send(0)
-    fill("q", "dn", 16, 7)
-    fill("s", "dn", 56, 4, "dz8")
-    for u in (24, 28, 32):
+    op("q", lambda: g.affine_select(T.cn[:, 0:CQ], T.ci[:, 0:CQ], [[0, CQ]], A.is_ge, 0.0, 0, 0), ["ci"], ["cn0"])
+    fill("q", "dn", 20, 1)
+    for i, u in enumerate((56, 52, 48)):
+        fill("s", "dn", u, 4, "dz%d" % (18 + i))
+    fill("s", "dn", 46, 2, "dz21")
+    for u in (24, 28):
         fill("a", "dn", u, 4)
-    fill("a", "dn", 53, 3)
-    fill("v", "dn", 14, 2)
-    fill("v", "dn", 36, 4)
-    op("v", lambda: v.tensor_scalar(T.cn[:], T.ci[:], -1.0, None, A.mult), ["ci"], ["cn"])
-    fill("v", "dn", 23, 1)
-    for u in range(40, 52, 4):
+    fill("a", "dn", 32, 3)
+    fill("v", "dn", 16, 2)
+    op("v", lambda: v.tensor_copy(T.cn[:, CQ:4 * U], T.ci[:, CQ:4 * U]), ["ci"], ["cn1"])
+    fill("v", "dn", 18, 2)
+    fill("v", "dn", 21, 3)
+    fill("v", "dn", 35, 1)
+    for u in (36, 40):
         fill("v", "dn", u, 4)
-    fill("v", "dn", 52, 1)
-    op("v", lambda: v.tensor_copy(T.idh[:], T.idb[:]), ["idb"], ["idh"])
-    op("v", lambda: v.memset(T.cc[:], C), [], ["cc"])
-    costs("dn", (0, 1, 2, 3, 9, 6, 10, 7, 11, 8, 12, 14, 4, 5, 13, 15))
+    fill("v", "dn", 44, 2)
+    costs("dn", (0, 1, 2, 3, 6, 4, 14, 7, 5, 13, 9, 12, 8, 10, 11))
+    costs("dn", (15,), "a")
+    op("a", lambda: a.activation(T.bm[:], T.b1[:], F.Copy, scale=-1.0), ["b1"], ["bm"])
     dma("s", T.dri[:, V:3 * V], T.drv[:, V:3 * V], [], ["dri1"], "dd1")
-    op("q", lambda: g.iota(T.wsb[:], [[0, V // G], [255, G]], int(MID) - 255 * (G - 1), 0, allow_small_or_imprecise_dtypes=True), [], ["wsb"])
-    fill("q", "zt", NU - 4, 4)
-    fill("q", "zt", 0, 16)
-    for i in range(8):
-        fill("s", "zt", 16 + 4 * i, 4, "dz%d" % i)
+    seed("zt", "q")
+    fill("q", "zt", NU - 3, 1)
+    fill("q", "zt", NU - 2, 2)
+    op("q", lambda: g.affine_select(T.drb[:], T.dri[:, V:2 * V], [[0, V]], A.is_ge, 0.0, 0, 0), ["dri1"], ["drb"])
+    op("q", lambda: g.affine_select(T.nid[:], T.idb[:], [[-1, 128]], A.not_equal, -1.0, 0, 1), ["idb"], ["nid"])
+    op("q", lambda: g.affine_select(T.id32[:], T.idb[:], [[0, 128]], A.is_ge, 0.0, 0, 0), ["idb"], ["id32"])
+    for u in range(0, 16, 4):
+        fill("q", "zt", u, 4)
+    fill("q", "zt", 56, 2)
+    for i in range(18):
+        fill("s", "zt", 16 + 2 * i, 2, "dz%d" % i)
     op("a", lambda: a.activation(T.fl[:], T.fi[:], F.Exp, scale=LAM), ["fi"], ["fl"])
-    work(0, "s0 s1 i0-16 i0-16 i0-16 i0-16 i0-16 a0-2 v7-16 a2-7 e0-2 e2-4 n x0-2 e4-8 x2-4 e8-12 x4-8 e12-16 c n n x8-16 n")
-    for u in range(48, NU - 4, 4):
-        fill("a", "zt", u, 4)
-    costs("zt", (4, 5, 6, 7, 12, 8, 13, 9, 14, 10, 11, 0, 1, 2, 3, 15))
-    scan()
+    work(0, "s0 s1 n i0-16 d i0-16 i0-16 i0-16 i0-16 a0-2 v8-16 a2-8 e0-2 e2-4 x0-2 e4-8 x2-4 e8-12 x4-8 e12-16 c n x8-16")
+    maxima(52)
+    scan(lambda: fill("a", "zt", 58, 2))
+    costs("zt", (4, 5, 6, 0, 7, 8, 1, 9, 10, 13, 2, 11, 12, 3, 14, 15))
     choose(1)
     send(1)
-    work(1, "c s0 n i0-2 n v0-2 e0-2 i0-2 n i0-2 n i0-2 i0-2 s1 i2-8 a4-8 i2-8 v2-4 i2-8 e2-4 e4-8 x0-2 i2-8 s2 i2-8 i8-16 a8-12 e8-12 "
-            "x2-4 i8-16 i8-16 a12-16 e12-16 x4-8 i8-16 i8-16 x8-12 x12-16")
+    work(1, "c s0 i0-2 a1-2 v0-1 e0-2 n n i0-2 n i0-2 n i0-2 n i0-2 n s1 i2-8 a2-4 a4-6 e2-4 a6-8 e4-6 i2-8 i2-8 x0-2 i2-8 s2 "
+            "i2-8 i8-16 a8-10 e6-8 a10-12 e8-10 a12-14 e10-12 a14-16 e12-14 e14-16 i8-16 x2-4 i8-16 x4-6 i8-16 x6-8 i8-16 x8-10 x10-12 "
+            "x12-14 x14-16")
     need("s", dict(cnt))
     op("a", lambda: a.activation(T.l32[:], T.la[:], F.Copy), ["la"], ["l32"])
     scan()
@@ -340,5 +416,7 @@ def rank_program(g, core, T, topo):
     dma("s", T.yx[:], T.x32[:], ["x32"], [], "dyx")
     choose(2)
     op("v", lambda: v.tensor_copy(T.l32[:, 0:L].indirect(T.raw[:, 0:2]), T.v32[:]), ["raw", "v32"], ["l32"])
+    need("s", {e: cnt[e] for e in "ap"})
     dma("s", T.yl[:], T.l32[:, 0:V], ["l32"], [], "dyl")
+    need("s", {"dyx": cnt["dyx"]})
     need("s", dict(cnt))

import math
from concourse.bass import DstId, RemoteDMATransfer
from concourse.mybir import AluOpType as A, AxisListType, ActivationFunctionType as F

N, V, CAP, RO, DEC = 8, 256, 32, 3, 24
W = V * 128
H = W // 2
G = 32
L = V + CAP
S = N * CAP
STEPS, LIFT, LOW, DOWN = 71.0, 8811.0, -8161.0, 68
LAM = math.log(2.0) / STEPS
C = 12582912.0
X, K, Q = 16639.5, 64.0 / 32769.0, 32769.0
B = 63.25 + 64.0 * X - 32.0 * Q
PIECES = ((0, 96), (96, 224), (224, 256))
PARTS = (((0, 1), (1, 8)), ((0, 1), (1, 4), (4, 8)))
E = PIECES[-1][0]
CQ = 768
U = 512
F32, BF, I32, U16, F16 = "float32", "bfloat16", "int32", "uint16", "float16"

SCRATCH = {}
for _n, _m, _t in (
        ("x0i", V, I32), ("dri", RO * V, I32), ("thi", 1, I32), ("thf", 1, F32), ("thn", 1, F32), ("thp", 1, F32), ("fani", 2048, I32),
        ("ci", 2048, I32), ("cn", 2048, BF), ("ones", L, BF), ("bt", 128, BF), ("b1", 128, BF), ("b2", 128, BF), ("bm", 128, BF),
        ("idb", 128, BF), ("nid", 128, BF), ("drb", V, BF), ("r1", V, BF), ("r2", V, BF), ("hh", S, F32), ("id32", 128, F32), ("ntc", V, F32), ("mms", V, BF), ("mls", V, BF),
        ("idh", 128, F16), ("cm", 1, F32), ("dn", W, BF), ("zt", W, BF), ("so", H, BF), ("cc", 1, F32), ("fi", 1, F32),
        ("fl", 1, BF), ("pi", 2, I32), ("jc", 1, BF), ("jb", 1, F32), ("jd", 1, F32), ("xe", L, BF), ("la", L, BF), ("a0", V, BF), ("mx", V, BF),
        ("ln", V, F32), ("rr", V, F32), ("chg", L, BF), ("cum", L, BF), ("le", L + 1, BF), ("sg", L, BF), ("acc", 2, F32), ("cb", 2, F32),
        ("tt2", 2, F32), ("raw", 2, U16), ("sb0", CAP + 2, F16), ("sb1", CAP + 2, F16), ("ids", S // 16, U16), ("w", S, F32), ("dd", S, F32),
        ("es", S, U16), ("of", S, U16), ("gm", 16 * S, BF), ("en", 16 * S, BF), ("l32", L, F32), ("x32", V, F32), ("v32", CAP, F32)):
    SCRATCH[_n] = ("sbuf", [128, _m], _t)
SCRATCH["sd"] = ("sbuf", [128, V // G, G], BF)
for _n in ("land0", "land1"):
    SCRATCH[_n] = ("sbuf", [128, N - 1, CAP + 2], F16)
for _n, _m in (("pc0", 1024), ("pc1", 1024), ("ps", 512), ("pt", 512), ("pv", 512), ("pa", 512)):
    SCRATCH[_n] = ("psum", [128, _m], F32)
DMAS = ["dx", "dd0", "dth", "dfan", "dd1", "dyx", "dyl", "dc", "ddn", "dzt"] + ["dz%d" % u for u in range(22)]
SEMAPHORES = ["v", "a", "p", "q"] + ["%s%d_%d" % (n, k, p) for n in ("arr", "sent") for k in range(2) for p in range(1, len(PARTS[k]))] + DMAS


def rank_program(g, core, T, topo):
    r = T.rank_of(core)
    if r is None:
        return
    eng = {"v": g.vector, "a": g.scalar, "p": g.tensor, "q": g, "s": g.sync}
    cnt, lw, lr, seen = {}, {}, {}, {e: {} for e in eng}

    def need(e, deps):
        for s in sorted(deps):
            if seen[e].get(s, 0) < deps[s]:
                eng[e].wait_ge(T.sem[s], deps[s])
                seen[e][s] = deps[s]

    def op(e, fn, rd, wr, sem=None, inc=1):
        deps = {}
        for k in rd:
            if k in lw:
                s, c = lw[k]
                deps[s] = max(deps.get(s, 0), c)
        for k in wr:
            if k in lw and not (e == "p" and lw[k][0] == "p"):
                s, c = lw[k]
                deps[s] = max(deps.get(s, 0), c)
            for s, c in lr.get(k, {}).items():
                deps[s] = max(deps.get(s, 0), c)
        need(e, deps)
        ins = fn()
        s = sem or e
        cnt[s] = cnt.get(s, 0) + inc
        ins.then_inc(T.sem[s], inc)
        for k in rd:
            lr.setdefault(k, {})[s] = cnt[s]
        for k in wr:
            lw[k] = (s, cnt[s])
            lr[k] = {}

    v, a, t = g.vector, g.scalar, g.tensor
    NU = W // U
    sdk = ["sd0", "sd1", "sd2"]

    def uk(tab, u=0, n=NU):
        return ["%s%d" % (tab, i) for i in range(u, u + n)]

    def pk(name):
        return ["%s%d" % (name, c) for c in range(len(PIECES))]

    def sk(name, lo, hi):
        return ["%s_%d" % (name, i) for i in range(lo // 16, (hi + 15) // 16)]

    def dma(e, out, in_, rd, wr, sem):
        op(e, lambda: eng[e].dma_start(out, in_), rd, wr, sem, 16)

    def fill(e, tab, u, n, sem=None):
        out, src, ks = T[tab][:, u * U:(u + n) * U], T[tab][:, W - 4 * U:W - (4 - n) * U], uk(tab, NU - 4, n)
        if e == "q":
            op("q", lambda: g.affine_select(out, src, [[0, n * U]], A.is_ge, 0.0, 0, 0), ks, uk(tab, u, n))
        elif e == "v":
            op("v", lambda: v.tensor_copy(out, src), ks, uk(tab, u, n))
        elif e == "a":
            op("a", lambda: a.activation(out, src, F.Copy), ks, uk(tab, u, n))
        else:
            dma("s", out, src, ks, uk(tab, u, n), sem)

    def seed(tab, e):
        for i in range(2):
            out = T[tab][:, W - 4 * U + i * V:W - 4 * U + (i + 1) * V]
            fn = (lambda: v.tensor_copy(out, T.sd[:])) if e == "v" else (lambda: g.affine_select(out, T.sd[:], [[0, V]], A.is_ge, 0.0, 0, 0))
            op(e, fn, sdk, uk(tab, NU - 4, i))

    def costs(tab, blocks, e="s"):
        for c in blocks:
            dma(e, T[tab][c::16, 4 * U * c:4 * U * (c + 1)], T.cn[c::16, :], ["cn0", "cn1"], uk(tab, 4 * c, 4), "d" + tab)

    def choose(k):
        if k == 0:
            op("v", lambda: v.tensor_tensor_scan(T.cum[:], T.chg[:], T.chg[:], 0.0, A.add, A.max), pk("chg") + ["chp"], ["cum"])
        else:
            op("v", lambda: v.tensor_tensor_scan(T.cum[:], T.chg[:], T.ones[:], 0.0, A.add, A.add), pk("chg") + ["chp", "ones", "none"], ["cum"])
        op("a", lambda: a.activation(T.sg[:], T.cum[:], F.Sign, bias=T.jb[:, 0:1], scale=-1.0, accum_out=T.acc[:, 0:1]), ["cum", "jb"], ["sg", "acc0"])
        if k == 0:
            op("a", lambda: a.activation(T.le[:, 0:L], T.cum[:], F.Sign, bias=T.jd[:, 0:1], scale=-1.0, accum_out=T.acc[:, 1:2]), ["cum", "jd"], ["le", "acc1"])
            fill("v", "dn", 12, 4)
        else:
            op("v", lambda: v.tensor_scalar(T.le[:, 0:L], T.cum[:], T.jc[:, 0:1], 2.0, A.is_le, A.mult), ["cum", "jc"], ["le"])
            op("v", lambda: v.tensor_reduce(T.acc[:, 1:2], T.le[:], AxisListType.X, A.add), ["le", "lel"], ["acc1"])
        acc = ["acc0", "acc1"]
        if k == RO - 1:
            op("v", lambda: v.tensor_scalar(T.raw[:], T.acc[:], 0.5, L / 2.0, A.mult, A.add), acc, ["raw"])
            op("v", lambda: v.tensor_copy(T.v32[:], T.xe[:, 0:L].indirect(T.raw[:, 0:2])), pk("x") + ["xp", "raw"], ["v32"])
            return
        sb = T["sb%d" % k]
        op("v", lambda: v.tensor_scalar(T.tt2[:], T.acc[:], float(2 * V - L), -float(V), A.is_ge, A.mult), acc, ["tt2"])
        op("v", lambda: v.tensor_scalar(T.cb[:], T.acc[:], 0.5, L / 2.0 + V * r, A.mult, A.add), acc, ["cb"])
        op("v", lambda: v.tensor_scalar(T.raw[:], T.acc[:], 0.5, L / 2.0, A.mult, A.add), acc, ["raw"])
        op("v", lambda: v.tensor_tensor(sb[:, CAP:CAP + 2], T.cb[:], T.tt2[:], A.add), ["cb", "tt2"], ["sbi%d" % k])
        op("v", lambda: v.tensor_copy(sb[:, 0:CAP], T.xe[:, 0:L].indirect(T.raw[:, 0:2])), pk("x") + ["xp", "raw"], ["sbv%d" % k])

    def send(k):
        need("q", {"v": max(lw["sbv%d" % k][1], lw["sbi%d" % k][1])})
        for p, (lo, hi) in enumerate(PARTS[k][1:], 1):
            ids, dsts, n, name = [], [], 0, "%d_%d" % (k, p)
            for s in range(lo, hi):
                rid, pid, _ = topo.addr(T.cores[(r + s) % N])
                ids.append(DstId(rid=rid, pnc=pid))
                dsts.append(T["land%d" % k][:, s - 1, :])
                n += len(topo.engines(T.cores[(r - s) % N], core))
            peer = T.cores[(r + lo) % N]
            g.remote_dma_fused([RemoteDMATransfer(dst_ids=ids, dma_engine_mask=topo.mask(core, peer), remote_sem=T.sem["arr" + name],
                                                  srcs=[T["sb%d" % k][:]], dsts=dsts)], local_sem=T.sem["sent" + name])
            cnt["sent" + name] = len(topo.engines(core, peer))
            cnt["arr" + name] = n
            lw["land" + name] = ("arr" + name, n)

    def sources(k, p):
        s0, s1 = PARTS[k][p]
        src, key = (T["land%d" % k][:, s0 - 1:s1 - 1, CAP:CAP + 2], "land%d_%d" % (k, p)) if p else (T["sb%d" % k][:, CAP:CAP + 2], "sbi%d" % k)
        op("v", lambda: v.tensor_copy(T.ids[:, 2 * s0:2 * s1], src), [key], sk("ids", CAP * s0, CAP * s1))

    def index(lo, hi, aside):
        ids, es, w, d = T.ids[:, lo // 16:hi // 16], T.es[:, lo:hi], T.w[:, lo:hi], T.dd[:, lo:hi]
        h, hk = (T.pa[:, lo:hi], ["pa"]) if aside else (T.pv[:, lo:hi], sk("h", lo, hi))

        def rounded():
            if aside:
                op("a", lambda: a.activation(T.hh[:, lo:hi], w, F.Identity, bias=T.cc[:, 0:1]), sk("w", lo, hi) + ["cc"], ["hh"])
                op("a", lambda: a.activation(h, T.hh[:, lo:hi], F.Identity, bias=-C), ["hh"], hk)
            else:
                op("v", lambda: v.tensor_scalar(h, w, C, C, A.add, A.subtract), sk("w", lo, hi), hk)

        return iter([
            lambda: op("v", lambda: v.tensor_copy(es, T.fani[:, 0:2048].indirect(ids)), ["fan"] + sk("ids", lo, hi), sk("es", lo, hi)),
            lambda: op("v", lambda: v.tensor_scalar(w, es, X, K, A.subtract, A.mult), sk("es", lo, hi), sk("w", lo, hi)),
            rounded,
            lambda: op("v", lambda: v.tensor_tensor(d, w, h, A.subtract), sk("w", lo, hi) + hk, sk("d", lo, hi)),
            lambda: op("v", lambda: v.tensor_scalar(T.of[:, lo:hi], d, Q, B, A.mult, A.add), sk("d", lo, hi), sk("of", lo, hi))])

    def gather(k, e, lo, hi):
        tab = ("dn", "zt")[k]
        out, win = T.gm[:, 16 * lo:16 * hi], T[tab][:, 0:W].indirect(T.es[:, lo:hi])
        fn = (lambda: v.tensor_copy(out, win)) if e == "v" else (lambda: a.activation(out, win, F.Copy))
        op(e, fn, uk(tab) + sk("es", lo, hi), sk("gm", lo, hi))

    turn = [0]

    def code(k, lo, hi):
        nb = (hi - lo) // CAP
        e0, e1, per = 16 * lo, 16 * hi, 16 // nb
        p = [p for p, (s0, s1) in enumerate(PARTS[k]) if s0 * CAP <= lo][-1]
        val, vk = (T["land%d" % k][:, lo // CAP - 1:hi // CAP - 1, 0:CAP], "land%d_%d" % (k, p)) if lo else (T["sb%d" % k][:, 0:CAP], "sbv%d" % k)
        banks = [(turn[0] + b) % 4 for b in range(nb)]
        turn[0] += nb
        at = [(T["pc%d" % (m // 2)], 512 * (m % 2), "pc%d%d" % (m // 2, m % 2)) for m in banks]
        for pc, o, key in at:
            for j in range(per):
                op("p", lambda: t.matmul(pc[:, o + j:o + 512:per], T.idh[:], val, j == 0, False), ["idh", vk], [key])
        for b, (pc, o, key) in enumerate(at):
            op("p", lambda: t.matmul(pc[:, o:o + 512], T.bm[:], T.gm[:, e0 + b:e1:nb], False, True), ["bm"] + sk("gm", lo, hi), [key])
        for b, (pc, o, key) in enumerate(at):
            op("a", lambda: a.activation(T.en[:, e0 + b:e1:nb], pc[:, o:o + 512], F.Exp, bias=LIFT * LAM, scale=LAM), [key], sk("en%d" % b, lo, hi))

    def scatter(lo, hi):
        op("v", lambda: v.tensor_copy(T.dn[:, 0:W].indirect(T.of[:, lo:hi]), T.en[:, 16 * lo:16 * hi]),
           sk("of", lo, hi) + sk("en0", lo, hi) + sk("en1", lo, hi), uk("dn"))

    def work(k, order):
        rows, nxt = {}, after(k)
        for x in order.split():
            if x == "n":
                next(nxt)()
            elif x == "c":
                scalars(k)
            elif x == "d":
                op("v", lambda: v.tensor_copy(T.idh[:], T.idb[:]), ["idb"], ["idh"])
            elif x[0] == "s":
                sources(k, int(x[1]))
            else:
                lo, hi = [16 * int(m) for m in x[1:].split("-")]
                if x[0] in "ij":
                    if x not in rows:
                        rows[x] = index(lo, hi, x[0] == "j")
                    next(rows[x])()
                elif x[0] == "e":
                    code(k, lo, hi)
                elif x[0] == "x":
                    scatter(lo, hi)
                else:
                    gather(k, x[0], lo, hi)

    def sums(c):
        lo, hi = PIECES[c]
        key = "ps" if hi <= E else "pa"
        ps = T[key][:, lo:hi]
        op("p", lambda: t.matmul(ps, T.bm[:], T.la[:, lo:hi], True, False), ["bm", "la"], [key])
        op("p", lambda: t.matmul(ps, T.bm[:], T.xe[:, lo:hi], False, False), ["bm", "x%d" % c], [key])
        op("p", lambda: t.matmul(ps, T.b2[:], T.mx[:, lo:hi], False, True), ["b2", "mx%d" % c], [key])
        if hi <= E:
            op("a", lambda: a.activation(T.chg[:, lo:hi], ps, F.Sign, bias=T.thn[:, 0:1]), [key, "thn"], ["chg%d" % c])
        else:
            op("v", lambda: v.tensor_scalar(T.chg[:, lo:hi], ps, T.thf[:, 0:1], 2.0, A.is_ge, A.mult), [key, "thf"], ["chg%d" % c])
        if c == 0:
            op("a", lambda: a.activation(T.chg[:, V:L], T.ps[:, 0:CAP], F.Sign, bias=T.thp[:, 0:1], scale=-1.0), ["ps", "thp"], ["chp"])

    def scan(between=None):
        def run(u):
            lo, hi = 64 * G * u, 64 * G * (u + 1)
            op("v", lambda: v.tensor_tensor_scan(T.so[:, lo:hi], T.dn[:, lo:hi], T.dn[:, H + lo:H + hi], T.fl[:, 0:1], A.max, A.max),
               uk("dn") + ["fl"], ["so%d" % u])

        def read(c):
            lo, hi = PIECES[c]
            op("a", lambda: a.activation(T.ln[:, lo:hi], T.so[:, 64 * lo + 63:64 * hi:64], F.Ln, scale=2.0 ** -DOWN),
               ["so%d" % u for u in range(lo // G, hi // G)], ["ln%d" % c])
            if hi <= E:
                op("a", lambda: a.activation(T.rr[:, lo:hi], T.ln[:, lo:hi], F.Identity, bias=T.cc[:, 0:1], scale=1.0 / LAM), ["ln%d" % c, "cc"], ["rr%d" % c])

        def level(c):
            lo, hi = PIECES[c]
            if hi <= E:
                pc, key = T["pc%d" % c][:, 0:hi - lo], "pc%d0" % c
                op("p", lambda: t.matmul(pc, T.id32[:], T.ntc[:, lo:hi], True, False), ["id32", "ntc"], [key])
                op("p", lambda: t.matmul(pc, T.id32[:], T.rr[:, lo:hi], False, True), ["id32", "rr%d" % c], [key])
            else:
                op("v", lambda: v.tensor_scalar(T.rr[:, lo:hi], T.ln[:, lo:hi], 1.0 / LAM, C, A.mult, A.add), ["ln%d" % c], ["rr%d" % c])
                op("v", lambda: v.tensor_tensor(T.a0[:, lo:hi], T.rr[:, lo:hi], T.pt[:, lo:hi], A.subtract), ["rr%d" % c, "tc"], ["a0"])

        def state(c):
            lo, hi = PIECES[c]
            lv, key, mm, ml = (T["pc%d" % c][:, 0:hi - lo], "pc%d0" % c, T.mms[:, lo:hi], T.mls[:, lo:hi]) if hi <= E else (
                T.a0[:, lo:hi], "a0", T.pt[:, V + lo:V + hi], T.pv[:, V + lo:V + hi])
            op("v", lambda: v.tensor_tensor(T.xe[:, lo:hi], lv, mm, A.max), [key, "mm", "mms"], ["x%d" % c])
            op("v", lambda: v.tensor_tensor(T.mx[:, lo:hi], lv, ml, A.max), [key, "ml", "mls"], ["mx%d" % c])
            sums(c)

        todo = {}
        for c, (lo, hi) in enumerate(PIECES):
            last = hi // G - 1
            todo.setdefault(last, []).insert(0, (read, c))
            todo.setdefault(last + (0, 0, 1)[c], []).append((level, c))
            todo.setdefault(last + (4, 1, 1)[c], []).append((state, c))
        for u in range(max(todo) + 1):
            if u < V // G:
                run(u)
            for f, c in todo.get(u, []):
                f(c)
                if between and (f, c) == (read, 0):
                    between()

    def scalars(k):
        if k == 1:
            op("a", lambda: a.activation(T.pa[:, 0:V], T.xe[:, 0:V], F.Identity, bias=-float(DEC)), pk("x"), ["pa"])
        if k == 0:
            op("a", lambda: a.activation(T.cm[:], T.cc[:], F.Identity, bias=LIFT - DOWN * STEPS), ["cc"], ["cm"])
            op("a", lambda: a.activation(T.b2[:], T.b1[:], F.Copy, scale=2.0), ["b1"], ["b2"])
            op("a", lambda: a.activation(T.pt[:, 0:V], T.sd[:], F.Identity, bias=T.cm[:, 0:1], scale=-15.0), sdk + ["cm"], ["tc", "mm"])
            op("a", lambda: a.activation(T.ntc[:], T.pt[:, 0:V], F.Copy, scale=-1.0), ["tc"], ["ntc"])
            op("a", lambda: a.activation(T.ones[:, E:V], T.b1[:, 0:V - E], F.Copy, scale=0.0), ["b1", "ones"], ["none"])
            op("a", lambda: a.activation(T.jc[:], T.jd[:], F.Identity, bias=-1.0), ["jd"], ["jc"])
            op("a", lambda: a.activation(T.thn[:], T.thf[:], F.Identity, bias=0.5, scale=-1.0), ["thf"], ["thn"])
            op("a", lambda: a.activation(T.thp[:], T.thf[:], F.Identity, bias=-0.5), ["thf"], ["thp"])

    def maxima(u):
        x, la = (T.xe[:, 0:V], pk("x")), (T.la[:, 0:V], ["la"])
        dr, r1, r2 = (T.drb[:], ["drb"]), (T.r1[:], ["r1"]), (T.r2[:], ["r2"])
        for i, (plus, minus, out, func, bias, ks) in enumerate((
                ([x], [dr], T.r1[:], F.Relu, -float(DEC), ["r1"]), ([r1, dr], [], T.pt[:, V + E:2 * V], F.Copy, 0.0, ["mm"]),
                ([r1, dr], [la], T.r2[:], F.Relu, 0.0, ["r2"]), ([r2, la], [], T.pv[:, V + E:2 * V], F.Copy, 0.0, ["ml"] + sk("h", 0, S)))):
            terms = [(T.idb, "idb", m) for m in plus] + [(T.nid, "nid", m) for m in minus]
            for j, (sign, key, (src, rd)) in enumerate(terms):
                op("p", lambda: t.matmul(T.pa[:, 0:V], sign[:], src, j == 0, j + 1 == len(terms)), [key] + rd, ["pa"])
            fill("a", "zt", u + i, 1)
            if i % 2:
                op("a", lambda: a.activation(T[ks[0] + "s"][:, 0:E], T.pa[:, 0:E], func), ["pa"], [ks[0] + "s"])
                op("a", lambda: a.activation(out, T.pa[:, E:V], func), ["pa"], ks)
            else:
                op("a", lambda: a.activation(out, T.pa[:, 0:V], func, bias=bias), ["pa"], ks)

    def after(k):
        lo, hi = (k + 1) * V, (k + 2) * V
        return iter([
            lambda: op("v", lambda: v.tensor_copy(T.la[:, 0:L].indirect(T.raw[:, 0:2]), T["sb%d" % k][:, 0:CAP]), ["raw", "sbv%d" % k], ["la"]),
            lambda: op("av"[k], lambda: (v.tensor_copy(T.xe[:, V:L], T.la[:, 0:CAP]) if k else a.activation(T.xe[:, V:L], T.la[:, 0:CAP], F.Copy)),
                       ["la"], ["xp"]),
            lambda: op("v", lambda: v.tensor_tensor(T.mms[:, 0:E], T.pa[:, 0:E], T.dri[:, lo:lo + E], A.max), ["pa", "dri1"], ["mms"]),
            lambda: op("v", lambda: v.tensor_tensor(T.pt[:, V + E:2 * V], T.pa[:, E:V], T.dri[:, lo + E:hi], A.max), ["pa", "dri1", "tc"], ["mm"]),
            lambda: op("v", lambda: v.tensor_tensor(T.mls[:, 0:E], T.mms[:, 0:E], T.la[:, 0:E], A.max), ["mms", "la"], ["mls"]),
            lambda: op("v", lambda: v.tensor_tensor(T.pv[:, V + E:2 * V], T.pt[:, V + E:2 * V], T.la[:, E:V], A.max), ["mm", "la"], ["ml"])])

    dma("s", T.x0i[:], T.x0[:], [], ["x0i"], "dx")
    dma("a", T.dri[:, 0:V], T.drv[:, 0:V], [], ["dri0"], "dd0")
    dma("s", T.thi[:], T.th[:], [], ["thi"], "dth")
    dma("s", T.ci[:], T.cost[:], [], ["ci"], "dc")
    dma("s", T.fani[:], T.fan[:], [], ["fan"], "dfan")

    op("q", lambda: g.iota(T.sd[:, :, 16:G], [[0, V // G], [-17, 16]], 255, 0, allow_small_or_imprecise_dtypes=True), [], ["sd2"])
    op("q", lambda: g.iota(T.sd[:, :, 1:16], [[0, V // G], [-18, 15]], 524, 0, allow_small_or_imprecise_dtypes=True), [], ["sd1"])
    op("v", lambda: v.memset(T.sd[:, :, 0], 544.0), [], ["sd0"])
    op("v", lambda: v.memset(T.ones[:], 1.0), [], ["ones"])
    op("q", lambda: g.iota(T.pi[:, 0:1], [[0, 1]], 0, 1), [], ["pi0"])
    op("q", lambda: g.affine_select(T.bt[:], T.ones[:, 0:128], [[-16, 8], [0, 16]], A.is_ge, 0.0, 0, 1), ["ones"], ["bt"])
    op("q", lambda: g.affine_select(T.b1[:], T.bt[:], [[16, 8], [0, 16]], A.is_ge, 0.0, 15, -1), ["bt"], ["b1"])
    op("v", lambda: v.memset(T.la[:], 0.0), [], ["la"])
    op("v", lambda: v.memset(T.xe[:, V:L], 0.0), [], ["xp"])
    op("v", lambda: v.memset(T.le[:, L:L + 1], -float(L)), [], ["lel"])
    op("v", lambda: v.memset(T.fi[:], LOW + LIFT), [], ["fi"])
    op("v", lambda: v.memset(T.cc[:], C), [], ["cc"])
    seed("dn", "v")
    op("v", lambda: v.tensor_scalar(T.pi[:, 1:2], T.pi[:, 0:1], 15, None, A.bitwise_and), ["pi0"], ["pi1"])
    fill("v", "dn", NU - 3, 1)
    op("v", lambda: v.tensor_scalar(T.jd[:], T.pi[:, 1:2], 2.0, 33.0, A.mult, A.add), ["pi1"], ["jd"])
    fill("v", "dn", NU - 2, 2)
    op("v", lambda: v.tensor_scalar(T.jb[:], T.pi[:, 1:2], 2.0, 1.0, A.mult, A.add), ["pi1"], ["jb"])
    fill("v", "dn", 0, 2)
    fill("a", "dn", 2, 1)
    fill("a", "dn", 3, 2)
    fill("a", "dn", 5, 3)
    fill("q", "dn", 8, 1)
    fill("q", "dn", 9, 2)
    op("q", lambda: g.affine_select(T.idb[:], T.ones[:, 0:128], [[-1, 128]], A.is_equal, 0.0, 0, 1), ["ones"], ["idb"])

    op("v", lambda: v.tensor_scalar(T.pv[:, 0:V], T.x0i[:], float(DEC), None, A.subtract), ["x0i"], sk("h", 0, S))
    op("v", lambda: v.tensor_copy(T.thf[:], T.thi[:]), ["thi"], ["thf"])
    op("v", lambda: v.tensor_tensor(T.xe[:, 0:V], T.pv[:, 0:V], T.dri[:, 0:V], A.max), sk("h", 0, S) + ["dri0"], pk("x"))
    op("p", lambda: t.matmul(T.ps[:, 0:V], T.b1[:], T.xe[:, 0:V], True, True), ["b1"] + pk("x"), ["ps"])
    fill("v", "dn", 11, 1)
    op("v", lambda: v.tensor_scalar(T.chg[:, 0:V], T.ps[:, 0:V], T.thf[:, 0:1], 2.0, A.is_ge, A.mult), ["ps", "thf"], pk("chg"))
    op("v", lambda: v.tensor_scalar(T.chg[:, V:L], T.ps[:, 0:CAP], T.thf[:, 0:1], 2.0, A.is_lt, A.mult), ["ps", "thf"], ["chp"])
    choose(0)
    send(0)
    op("q", lambda: g.affine_select(T.cn[:, 0:CQ], T.ci[:, 0:CQ], [[0, CQ]], A.is_ge, 0.0, 0, 0), ["ci"], ["cn0"])
    fill("q", "dn", 20, 1)
    for i, u in enumerate((56, 52, 48)):
        fill("s", "dn", u, 4, "dz%d" % (18 + i))
    fill("s", "dn", 46, 2, "dz21")
    for u in (24, 28):
        fill("a", "dn", u, 4)
    fill("a", "dn", 32, 3)
    fill("v", "dn", 16, 2)
    op("v", lambda: v.tensor_copy(T.cn[:, CQ:4 * U], T.ci[:, CQ:4 * U]), ["ci"], ["cn1"])
    fill("v", "dn", 18, 2)
    fill("v", "dn", 21, 3)
    fill("v", "dn", 35, 1)
    for u in (36, 40):
        fill("v", "dn", u, 4)
    fill("v", "dn", 44, 2)
    costs("dn", (0, 1, 2, 3, 6, 4, 14, 7, 5, 13, 9, 12, 8, 10, 11))
    costs("dn", (15,), "a")
    op("a", lambda: a.activation(T.bm[:], T.b1[:], F.Copy, scale=-1.0), ["b1"], ["bm"])
    dma("s", T.dri[:, V:3 * V], T.drv[:, V:3 * V], [], ["dri1"], "dd1")
    seed("zt", "q")
    fill("q", "zt", NU - 3, 1)
    fill("q", "zt", NU - 2, 2)
    op("q", lambda: g.affine_select(T.drb[:], T.dri[:, V:2 * V], [[0, V]], A.is_ge, 0.0, 0, 0), ["dri1"], ["drb"])
    op("q", lambda: g.affine_select(T.nid[:], T.idb[:], [[-1, 128]], A.not_equal, -1.0, 0, 1), ["idb"], ["nid"])
    op("q", lambda: g.affine_select(T.id32[:], T.idb[:], [[0, 128]], A.is_ge, 0.0, 0, 0), ["idb"], ["id32"])
    for u in range(0, 16, 4):
        fill("q", "zt", u, 4)
    fill("q", "zt", 56, 2)
    for i in range(18):
        fill("s", "zt", 16 + 2 * i, 2, "dz%d" % i)
    op("a", lambda: a.activation(T.fl[:], T.fi[:], F.Exp, scale=LAM), ["fi"], ["fl"])
    work(0, "s0 s1 n i0-16 d i0-16 i0-16 i0-16 i0-16 a0-2 v8-16 a2-8 e0-2 e2-4 x0-2 e4-8 x2-4 e8-12 x4-8 e12-16 c n x8-16")
    maxima(52)
    scan(lambda: fill("a", "zt", 58, 2))
    costs("zt", (4, 5, 6, 0, 7, 8, 1, 9, 10, 13, 2, 11, 12, 3, 14, 15))
    choose(1)
    send(1)
    work(1, "c s0 i0-2 a1-2 v0-1 e0-2 n n i0-2 n i0-2 n i0-2 n i0-2 n s1 i2-8 a2-4 a4-6 e2-4 a6-8 e4-6 i2-8 i2-8 x0-2 i2-8 s2 "
            "i2-8 i8-16 a8-10 e6-8 a10-12 e8-10 a12-14 e10-12 a14-16 e12-14 e14-16 i8-16 x2-4 i8-16 x4-6 i8-16 x6-8 i8-16 x8-10 x10-12 "
            "x12-14 x14-16")
    need("s", dict(cnt))
    op("a", lambda: a.activation(T.l32[:], T.la[:], F.Copy), ["la"], ["l32"])
    scan()
    op("a", lambda: a.activation(T.x32[:], T.xe[:, 0:V], F.Copy), pk("x"), ["x32"])
    dma("s", T.yx[:], T.x32[:], ["x32"], [], "dyx")
    choose(2)
    op("v", lambda: v.tensor_copy(T.l32[:, 0:L].indirect(T.raw[:, 0:2]), T.v32[:]), ["raw", "v32"], ["l32"])
    need("s", {e: cnt[e] for e in "ap"})
    dma("s", T.yl[:], T.l32[:, 0:V], ["l32"], [], "dyl")
    need("s", {"dyx": cnt["dyx"]})
    need("s", dict(cnt))
